import numpy as np, ml_dtypes
CORES = [3,11,19,27,35,43,51,59]
N = 8
BF = ml_dtypes.bfloat16
B, S, D, SH = 2, 8192, 4096, 5
W, BC = N * B, 16
LAST = (2 * 255 * 255) >> SH
def middle(m):
    return 16 * (m % 16) + 8, 16 * (m // 16) + 8
def index(p, x, y):
    return ((x - int(p[0])) ** 2 + (y - int(p[1])) ** 2) >> SH
def loud(d, rng, cells):
    t = rng.integers(0, S, (N, 8)); sg = rng.choice(np.array([-15.0, 15.0]), 16); v = d["tr"].reshape(N, 8, 16, S); x, y = middle(np.array(cells))
    ld = sg - np.sign(sg) * rng.integers(0, 2, (N, 8, 16))
    for q in range(N):
        for g in range(8):
            d["tau"][q, g, index(d["pos"][q, g], x, y)] = t[q, g]; v[q, g, :, t[q, g]] = ld[q, g].astype(BF)
    return t, ld
def setup_inputs(rng):
    tr = rng.integers(-15, 16, (N, 128, S), dtype=np.int8).astype(np.float32).astype(BF)
    pos = rng.integers(0, 256, (N, 8, 2)).astype(np.int32)
    t = np.floor(np.sqrt(np.arange(D) / D) * (rng.random((N, 8, 1)) * 0.5 + 0.25) * S).astype(np.int64) + rng.integers(0, S // 4, (N, 8, D))
    return {"tr": tr, "pos": pos, "tau": t.astype(np.int32)}
def setup_inputs_ends(rng):
    d = setup_inputs(rng); c = np.array([[0, 0], [0, 255], [255, 0], [255, 255]])
    d["pos"] = np.stack([c[rng.permutation(8) % 4] for q in range(N)]).astype(np.int32)
    t = rng.integers(0, S, (N, 8, D)); t[:, :, 0] = 0; t[:, :, LAST] = S - 1; d["tau"] = t.astype(np.int32)
    e = rng.integers(0, 2, W); e[0] = 0; e[W - 1] = 1
    loud(d, rng, np.arange(W) * BC + e * (BC - 1)); return d
def setup_inputs_ties(rng):
    d = setup_inputs(rng); s = int(rng.integers(0, 3)); cells = []
    for k in range(W):
        z = (k + s) % 3; o = [0, BC - 1] if z == 0 else rng.choice(BC, 2, replace=False) if z == 1 else range(BC)
        cells += [k * BC + int(i) for i in o]
    loud(d, rng, cells); return d
def setup_inputs_close(rng):
    d = setup_inputs(rng); k = np.arange(W); lo = k * BC + rng.integers(0, BC // 2, W); hi = k * BC + BC // 2 + rng.integers(0, BC // 2, W); x, y = middle(lo)
    d["pos"][k % N, k // N, 0] = x; d["pos"][k % N, k // N, 1] = y
    t, ld = loud(d, rng, np.concatenate([lo, hi])); v = d["tr"].reshape(N, 8, 16, S); m = np.abs(np.sum(ld, axis=(0, 1)))
    for i in range(W):
        q, g = i % N, i // N; u = (int(t[q, g]) + int(rng.integers(1, S))) % S; h = ld[q, g].copy(); s = int(rng.integers(0, 16))
        if i % 2:
            z = [(m[a] - m[b], a, b) for a in range(16) for b in range(16) if m[a] > m[b] + 1 and abs(h[b]) < 15]
            if z:
                s, b = min(z)[1:]; h[b] = h[b] + np.sign(h[b])
        h[s] = h[s] - np.sign(h[s])
        d["tau"][q, g, 0] = u; v[q, g, :, u] = h.astype(BF)
    return d
def setup_inputs_steps(rng):
    d = setup_inputs(rng); d["pos"] = np.repeat(rng.integers(0, 256, (N, 1, 2)), 8, axis=1).astype(np.int32)
    d["tau"] = np.repeat(rng.integers(0, S, (N, 8, D // 64)), 64, axis=2).astype(np.int32); return d
def setup_inputs_spread(rng):
    d = setup_inputs(rng); a = rng.choice(np.array([0, 1, 4, 15], np.int8), (N, 8, 1, S))
    v = np.clip(rng.integers(-15, 16, (N, 8, 16, S), dtype=np.int8), -a, a)
    d["tr"] = v.reshape(N, 128, S).astype(np.float32).astype(BF)
    d["pos"] = np.floor(256 * rng.random((N, 8, 2)) ** 3).astype(np.int32); d["tau"] = np.floor(S * rng.random((N, 8, D)) ** 3).astype(np.int32); return d
def check_inputs(d):
    bad = []; v = np.asarray(d["tr"]).astype(np.float32)
    if not ((np.abs(v) <= 15) & (np.rint(v) == v)).all(): bad.append("samples")
    if not ((d["pos"] >= 0) & (d["pos"] <= 255)).all(): bad.append("places")
    if not ((d["tau"] >= 0) & (d["tau"] < S)).all(): bad.append("times")
    return bad
def focus(v, pos, tau, x, y):
    a = np.zeros((16, len(x)), np.int64)
    for q in range(N):
        for g in range(8): a += v[q, g][:, tau[q, g][index(pos[q, g], x, y)]]
    return a
def reference(tr, pos, tau):
    v = tr.astype(np.float32).astype(np.int32).reshape(N, 8, 16, S)
    x, y = middle(np.arange(256)); c = focus(v, pos, tau, x, y)
    e = np.sum(c * c, axis=0).reshape(W, BC)
    w = np.arange(W) * BC + np.argmax(e, axis=1)
    j = np.arange(256); x = (16 * (w % 16)[:, None] + j % 16).reshape(-1); y = (16 * (w // 16)[:, None] + j // 16).reshape(-1)
    fine = focus(v, pos, tau, x, y).reshape(16, N, B * 256).transpose(1, 0, 2)
    return {"y": np.ascontiguousarray(fine).astype(np.float32), "w": np.tile(w.reshape(1, 1, W), (N, 1, 1)).astype(np.float32)}

@@ -1,0 +1,355 @@
+from concourse.bass import DstId, RemoteDMATransfer
+from concourse.mybir import AluOpType as A, ActivationFunctionType as F
+
+_SB = {
+    "int32": "posi 2 taus 256 vi 128 e8s 128 pgi 2 wdi 16 wdm 16 pcol 2 rcol 2 r4 2 d2w 16 lo32 16 d2i 256 hi 256",
+    "uint16": "tauo 256 lo 16 nl 16 flist 256",
+    "bfloat16": "posf 2 trs 8192 nat 4096 e8 128 ones 256 ident 128 wd 144 wf 80 vc 256 cland 256 xq 16 lxa 128 lxb 128 em 256 "
+                "dga 256 dgb 256 ff 4096 fsend 448 fland 512",
+    "float32": "negp 2 lw 140 pgf 2 pf 2 rf 2 c16 2 c4 2 dyw 2 yy 256 xx 256 yrot 256 sy 256 t1 16 sw 16 "
+               "hm 256 prod 256 dg 64 dd 64 a3 32 a4 16 dy2 256 dy2s 256 dx2 2 dxs 2 rfree 128 le 32 identf 128 sq 32 "
+               "one64 64 pw 260 tauf 256 taut 256 run 16 lt 16 acol 2 wc 16 w2 16 ysb 128",
+}
+SCRATCH = {"p%d" % _k: ("psum", [128, 512], "float32") for _k in range(8)}
+for _d in _SB:
+    _l = _SB[_d].split()
+    for _k in range(0, len(_l), 2):
+        SCRATCH[_l[_k]] = ("sbuf", [128, int(_l[_k + 1])], _d)
+SEMAPHORES = ["carr%d" % _k for _k in range(8)] + ["far%d" % _k for _k in range(5)] + ["csent", "fsent", "shared", "ssent"] + ["e%d" % _k for _k in range(130)]
+
+
+def rank_program(g, core, T, topo):
+    rank = T.rank_of(core)
+    if rank is None:
+        return
+    N = len(T.cores)
+    vec, sca, pe = g.vector, g.scalar, g.tensor
+    queues = {"G": g, "V": vec, "S": sca, "P": pe, "Y": g.sync}
+    known = {q: set() for q in queues}
+    events = []
+
+    def event():
+        e = {"n": len(events), "sem": T.sem["e%d" % len(events)], "total": 0, "knows": set(), "used": False}
+        events.append(e)
+        return e
+
+    def use(q, waits):
+        for e in waits:
+            if e["n"] not in known[q]:
+                queues[q].wait_ge(e["sem"], e["total"])
+                e["used"] = True
+                known[q] |= e["knows"] | {e["n"]}
+
+    def run(q, waits, call, ev=None, inc=1):
+        use(q, waits)
+        e = event() if ev is None else ev
+        assert not e["used"]
+        call().then_inc(e["sem"], inc)
+        e["total"] += inc
+        e["knows"] |= known[q]
+        return e
+
+    def V(waits, fn, *a, **k):
+        return run("V", waits, lambda: fn(*a), **k)
+
+    ts, tt, cp = vec.tensor_scalar, vec.tensor_tensor, vec.tensor_copy
+    act = lambda waits, out, in_, func, ev=None, **k: run("S", waits, lambda: sca.activation(out, in_, func, **k), ev=ev)
+
+    def chain(waits, mms):
+        use("P", waits)
+        for m in mms:
+            last = m()
+        return run("P", [], lambda: last)
+
+    p = [T["p%d" % k] for k in range(8)]
+
+    e_pos = run("Y", [], lambda: g.sync.dma_start(T.posi[0:8, :], T.pos[:, :]), inc=16)
+    e_tau = run("S", [], lambda: sca.dma_start(T.taus[:, :], T.tau[:, :]), inc=16)
+    e_tr = run("Y", [], lambda: g.sync.dma_start(T.trs[:, :], T.tr[:, :]), inc=16)
+
+    def kind(a, b):
+        a, b = topo.chip(T.cores[a]), topo.chip(T.cores[b])
+        return 2 if topo.mates(a, b) else 1 if topo.same_plane(a, b) else 0
+
+    def ordered(r):
+        return sorted([q for q in range(N) if q != r], key=lambda q: (kind(r, q), (q - r) % N)) + [r]
+
+    order = ordered(rank)
+    others, mate = order[:-1], order[-2]
+    senders = [[q for q in range(N) if ordered(q)[t] == rank][0] for t in range(N)]
+
+    def dst_id(q):
+        rid, pid, _ = topo.addr(T.cores[q])
+        return DstId(rid=rid, pnc=pid)
+
+    def bits(es):
+        m = 0
+        for e in es:
+            m |= 1 << e
+        return m
+
+    eng = [e for e in topo.engines(core, T.cores[mate]) if all(e in topo.engines(core, T.cores[q]) for q in others)]
+
+    runs, t = [], 0
+    while t < N:
+        n, d = 1, (order[t + 1] - order[t] if t + 1 < N else 1)
+        while t + n < N and order[t + n] == order[t] + n * d:
+            n += 1
+        runs.append((t, order[t], d, n))
+        t += n
+
+    iota_i = lambda out, pat, base, cm: run("G", [], lambda: g.iota(out, pat, base, cm))
+    iota_f = lambda out, pat, base, ev=None: run("G", [], lambda: g.iota(out, pat, base, 0, allow_small_or_imprecise_dtypes=True), ev=ev)
+    sel = lambda waits, out, in_, pat, op, base, cm, ev=None: run("G", waits, lambda: g.affine_select(out, in_, pat, op, 0.0, base, cm), ev=ev)
+    e_one64 = V([], vec.memset, T.one64[:, :], 1.0)
+    e_ones = V([], vec.memset, T.ones[:, :], 1.0)
+    e_wd0 = V([], vec.memset, T.wd[:, :], 0.0)
+    e_pw0 = V([], vec.memset, T.pw[:, :], 0.0)
+    e_tab0 = V([], vec.memset, T.wf[:, :] if rank < mate else T.le[:, :], 0.0)
+    e_pcol = iota_i(T.pcol[:, 0:1], [[1, 1]], 0, 1)
+    e_vi = iota_i(T.vi[:, :], [[1, 8], [16, 4], [0, 4]], 0, 0)
+    e_yy = iota_f(T.yy[:, :], [[0, 16], [16, 16]], 8)
+    e_xx = iota_f(T.xx[:, :], [[16, 16], [0, 16]], 8)
+    e_pw = event()
+    for o in range(2):
+        sel([e_one64, e_pw0], T.pw[:, 130 * o + 1:130 * o + 129:2], T.one64[:, :], [[-32, 4], [-1, 16]], A.is_equal, -16 * o, 1, ev=e_pw)
+    e_wdi = iota_i(T.wdi[:, :], [[1, 16]], 128, -1)
+    e_ident = sel([e_ones], T.ident[:, :], T.ones[:, 0:128], [[-1, 128]], A.is_equal, 0, 1)
+
+    e_r = V([e_pcol], ts, T.rcol[:, 0:1], T.pcol[:, 0:1], 15, None, A.bitwise_and)
+    e_pgi = V([], ts, T.pgi[:, 0:1], T.pcol[:, 0:1], 4, None, A.arith_shift_right)
+    e_pf = V([], cp, T.pf[:, 0:1], T.pcol[:, 0:1])
+    e_e8s = V([e_vi], ts, T.e8s[0:8, :], T.vi[0:8, :], 15, None, A.bitwise_and)
+    e_pgf = V([e_pgi], cp, T.pgf[:, 0:1], T.pgi[:, 0:1])
+    e_e8 = V([e_e8s, e_pf], ts, T.e8[0:8, :], T.e8s[0:8, :], T.pf[0:8, 0:1], -1.0, A.is_equal, A.mult)
+    e_c16 = V([e_r], ts, T.c16[:, 0:1], T.rcol[:, 0:1], 16.0, 8.0, A.mult, A.add)
+
+    e_posf = V([e_pos], cp, T.posf[0:8, :], T.posi[0:8, :])
+    e_pb = run("P", [e_e8, e_posf], lambda: pe.matmul(p[0][:, 0:2], T.e8[0:8, :], T.posf[0:8, :], start=True, stop=True))
+    e_rf = V([e_r], cp, T.rf[:, 0:1], T.rcol[:, 0:1])
+    e_xq = V([e_posf, e_ones], ts, T.xq[0:8, :], T.ones[0:8, 0:16], T.posf[0:8, 0:1], None, A.mult)
+    e_np = V([e_pb], cp, T.negp[:, :], p[0][:, 0:2])
+    nx, ny = T.negp[:, 0:1], T.negp[:, 1:2]
+    e_dyw = act([e_c16, e_np], T.dyw[:, 0:1], T.c16[:, 0:1], F.Square, bias=ny)
+    e_sy = act([e_yy], T.sy[:, :], T.yy[:, :], F.Square, bias=ny)
+    e_sx = act([e_xx], p[6][:, 0:256], T.xx[:, :], F.Square, bias=nx)
+    e_pq = run("P", [e_xq], lambda: pe.matmul(p[7][0:16, 0:128], T.xq[0:8, :], T.e8[0:8, :], start=True, stop=True))
+
+    e_t1 = V([e_yy, e_np], ts, T.t1[:, :], T.yy[:, 0:16], nx, None, A.add)
+    e_l = event()
+    V([], vec.memset, T.lw[:, 0:12], 0.0, ev=e_l)
+    e_sw = V([e_t1], tt, T.sw[:, :], T.t1[:, :], T.t1[:, :], A.mult)
+    V([e_vi, e_pgf], ts, T.lw[:, 12:140], T.vi[:, :], T.pgf[:, 0:1], None, A.is_equal, ev=e_l)
+    e_d2w = V([e_sw, e_dyw], ts, T.d2w[:, :], T.sw[:, :], T.dyw[:, 0:1], None, A.add)
+
+    e_tauf = V([e_tau], cp, T.tauf[:, :], T.taus[:, :])
+
+    def pairs(o):
+        use("P", [e_tauf, e_pw])
+        for x in range(2):
+            mm = pe.matmul(p[5][:, 128 * o:128 * o + 128], T.pw[:, 130 * o + 1 - x:130 * o + 129 - x], T.tauf[:, 128 * x:128 * x + 128],
+                           start=x == 0, stop=x == 1)
+        return run("P", [], lambda: mm)
+
+    pairs(0)
+    e_lo32 = V([e_d2w], ts, T.lo32[:, :], T.d2w[:, :], 5, 255, A.arith_shift_right, A.bitwise_and)
+    e_lo = V([e_lo32], cp, T.lo[:, :], T.lo32[:, :])
+    e_wdm = V([e_wdi], ts, T.wdm[:, :], T.wdi[:, :], 15, None, A.bitwise_and)
+    e_d2i = V([e_sx, e_sy], tt, T.d2i[:, :], p[6][:, 0:256], T.sy[:, :], A.add)
+    e_hi = V([e_d2i], ts, T.hi[:, :], T.d2i[:, :], 13, None, A.arith_shift_right)
+
+    e_shared = {"n": len(events), "sem": T.sem.shared, "total": len(eng), "knows": set(), "used": False}
+    events.append(e_shared)
+    if rank < mate:
+        e_made = V([e_wdm, e_tab0], ts, T.wf[:, 3:67:4], T.wdm[:, :], 0.0, None, A.is_equal)
+        e_wf, e_le, table = e_made, e_shared, T.wf
+    else:
+        e_made = event()
+        for h in range(2):
+            sel([e_l, e_tab0], T.le[:, 17 * h:17 * h + 15:2], T.lw[:, 12:140:16], [[0, 8]], A.is_equal, 0, 0, ev=e_made)
+        e_wf, e_le, table = e_shared, e_made, T.le
+    use("G", [e_made])
+    g.remote_dma_fused([RemoteDMATransfer(dst_ids=[dst_id(mate)], dma_engine_mask=bits(eng), remote_sem=T.sem.shared,
+                                          srcs=[table[:, :]], dsts=[table[:, :]])], local_sem=T.sem.ssent)
+    e_yrot = event()
+    for t, q, d, n in runs:
+        iota_f(T.yrot[:, 32 * t:32 * t + 32 * n], [[32 * d, n], [1, 32]], 32 * q, ev=e_yrot)
+    e_rfree = iota_f(T.rfree[0:16, :], [[0, 8], [1, 16]], 0)
+
+    e_hm = V([e_hi, e_rf], ts, T.hm[:, :], T.hi[:, :], T.rf[:, 0:1], None, A.is_equal)
+    e_prod = [V([e_hm, e_lo, e_tau], lambda k=k: tt(T.prod[:, 128 * k:128 * k + 128], T.taus[:, :].indirect(T.lo[:, 8 * k:8 * k + 8]),
+                                                    T.hm[:, 128 * k:128 * k + 128], A.mult)) for k in range(2)]
+    for q in range(4):
+        use("P", [e_prod[q // 2], e_l])
+        mm = pe.matmul(p[1][:, 0:64], T.lw[:, 12 - 4 * q:140 - 4 * q], T.prod[:, 64 * q:64 * q + 64], start=q == 0, stop=q == 3)
+    e_s = run("P", [], lambda: mm)
+    e_z = pairs(1)
+
+    e_dx2 = act([e_rf], T.dx2[:, 0:1], T.rf[:, 0:1], F.Square, bias=nx)
+    e_dxs = act([e_dx2], T.dxs[:, 0:1], T.dx2[:, 0:1], F.Copy, bias=-15.5 / 32, scale=1.0 / 32)
+    e_idf = act([e_ident], T.identf[:, :], T.ident[:, :], F.Copy)
+    e_dy2 = act([e_yrot], T.dy2[:, :], T.yrot[:, :], F.Square, bias=ny)
+    e_dy2s = act([e_dxs, e_dy2], T.dy2s[:, :], T.dy2[:, :], F.Identity, bias=T.dxs[:, 0:1], scale=1.0 / 32)
+    e_r4 = V([], ts, T.r4[:, 0:1], T.pcol[:, 0:1], 3, None, A.bitwise_and)
+    e_wd = V([e_wdm, e_wd0], ts, T.wd[:, 16:32], T.wdm[:, :], 0.0, None, A.is_equal)
+    e_c4 = V([e_r4], ts, T.c4[:, 0:1], T.r4[:, 0:1], 16.0, 8.0, A.mult, A.add)
+    e_dg = V([e_xx, e_c4], ts, T.dg[:, :], T.xx[:, 0:64], T.c4[:, 0:1], None, A.is_equal)
+    e_dd = V([e_s, e_dg], tt, T.dd[:, :], p[1][:, 0:64], T.dg[:, :], A.mult)
+    e_a3 = V([e_dd], tt, T.a3[:, :], T.dd[:, 0:32], T.dd[:, 32:64], A.add)
+    e_a4 = V([e_a3], tt, T.a4[:, :], T.a3[:, 0:16], T.a3[:, 16:32], A.add)
+    e_nl = V([e_a4], cp, T.nl[:, :], T.a4[:, :])
+
+    e_tt, e_tauo = event(), [None, None]
+    for k in range(8):
+        V([e_z], vec.transpose, T.taut[:, 32 * k:32 * k + 32], p[5][:, k:256:8], ev=e_tt)
+    for k in range(2):
+        e_tauo[k] = V([e_tt], cp, T.tauo[:, 128 * k:128 * k + 128], T.taut[:, 128 * k:128 * k + 128])
+
+    e_va = [act([e_tr, e_nl], T.vc[:, 64 * k:64 * k + 64], T.trs[:, :].indirect(T.nl[:, 4 * k:4 * k + 4]), F.Copy) for k in (0, 1)]
+    e_vv = [V([e_tr, e_nl], cp, T.vc[:, 64 * k:64 * k + 64], T.trs[:, :].indirect(T.nl[:, 4 * k:4 * k + 4])) for k in (2, 3)]
+    e_lxa = V([e_pq, e_rfree], tt, T.lxa[0:16, :], p[7][0:16, 0:128], T.rfree[0:16, :], A.add)
+    e_lxb = V([], vec.memset, T.lxb[0:16, :], 8.0)
+    use("P", [e_wd])
+    for k in (0, 1, 4, 5, 2, 3, 6, 7):
+        use("P", [(e_va + e_vv)[k // 2]])
+        o = 32 * (k // 2)
+        mm = pe.matmul(p[2][o:o + 32, 0:32], T.wd[:, 16 - 16 * (k % 2):48 - 16 * (k % 2)], T.vc[:, 32 * k:32 * k + 32], start=k % 2 == 0, stop=k % 2 == 1)
+    e_cs = run("P", [], lambda: mm)
+    own = slice(32 * rank, 32 * rank + 32)
+    e_own = V([e_cs], cp, T.cland[:, own], p[2][:, 0:32])
+    use("G", [e_own])
+    g.remote_dma_fused([RemoteDMATransfer(dst_ids=[dst_id(q) for q in others], dma_engine_mask=bits(eng), remote_sem=T.sem["carr%d" % rank],
+                                          srcs=[T.cland[:, own]], dsts=[T.cland[:, own] for q in others])], local_sem=T.sem.csent)
+    e_em = event()
+    for t, q, d, n in runs:
+        sel([e_ones], T.em[0:16, 32 * t:32 * t + 32 * n], T.ones[0:16, 0:32 * n], [[-2 * d, n], [-1, 2], [0, 16]], A.is_equal, -2 * q, 1, ev=e_em)
+    e_wc = iota_f(T.wc[0:1, :], [[16, 16]], 0)
+
+    e_n = {q: event() for q in "VS"}
+    for k in range(8):
+        q = "VS"[k // 4]
+        o, i = T.nat[:, k:4096:8], T.trs[:, :].indirect(T.tauo[:, 32 * k:32 * k + 32])
+        if q == "V":
+            V([e_tr, e_tauo[0]], cp, o, i, ev=e_n[q])
+        else:
+            act([e_tr, e_tauo[1]], o, i, F.Copy, ev=e_n[q])
+
+    use("P", [e_own, e_ident])
+    pe.matmul(p[3][:, 0:32], T.ident[:, :], T.cland[:, own], start=True, stop=False)
+    parts = [(0, 64), (64, 256)]
+    use("P", [e_idf, e_dy2s, e_lxa])
+    for k, (c0, c1) in enumerate(parts):
+        pe.matmul(p[6 + k][:, 0:c1 - c0], T.identf[:, :], T.dy2s[:, c0:c1], start=True, stop=False)
+    for q in senders[:-1]:
+        pe.wait_ge(T.sem["carr%d" % q], len(eng))
+        mm = pe.matmul(p[3][:, 0:32], T.ident[:, :], T.cland[:, 32 * q:32 * q + 32], start=False, stop=q == senders[N - 2])
+    e_tot = run("P", [], lambda: mm)
+    e_sq = act([e_tot], T.sq[:, :], p[3][:, 0:32], F.Square)
+    e_e = chain([e_sq, e_le], [lambda: pe.matmul(p[4][0:16, 0:16], T.le[:, 0:16], T.sq[:, 0:16], start=True, stop=False),
+                               lambda: pe.matmul(p[4][0:16, 0:16], T.le[:, 16:32], T.sq[:, 16:32], start=False, stop=True)])
+    e_run = V([e_e, e_one64], vec.tensor_tensor_scan, T.run[0:16, :], T.one64[0:16, 0:16], p[4][0:16, 0:16], 0.0, A.mult, A.max)
+    ac = T.acol[0:16, 0:1]
+    e_ac = act([e_run], T.lt[0:16, :], T.run[0:16, :], F.Sign, bias=T.run[0:16, 15:16], scale=-1.0, accum_out=ac)
+    e_d = []
+    for k, (c0, c1) in enumerate(parts):
+        e_a = V([e_ac, e_em], ts, T.dga[0:16, c0:c1], T.em[0:16, c0:c1], ac, None, A.mult)
+        e_b = act([e_ac, e_em], T.dgb[0:16, c0:c1], T.em[0:16, c0:c1], F.Square, scale=ac)
+        o = p[6 + k][:, 0:c1 - c0]
+        use("P", [e_a])
+        pe.matmul(o, T.lxa[0:16, :], T.dga[0:16, c0:c1], start=False, stop=False)
+        e_d.append(chain([e_b, e_lxb], [lambda: pe.matmul(o, T.lxb[0:16, :], T.dgb[0:16, c0:c1], start=False, stop=True)]))
+
+    e_sel = {}
+
+    def select(k):
+        t0, t1 = parts[k][0] // 32, parts[k][1] // 32
+        e = V([e_d[k]], cp, T.flist[:, 32 * t0:32 * t1], p[6 + k][:, 0:32 * (t1 - t0)])
+        for t in range(t0, t1):
+            e_sel[t] = e
+
+    groups = [[0], [1], [2, 3], [4, 5], [6]]
+    banks = [p[0], p[1], p[2], p[3], p[4]]
+    at = {t: (k, tts.index(t)) for k, tts in enumerate(groups) for t in tts}
+    e_f = {t: [] for t in range(N)}
+
+    def gather(q, t, j0=0, j1=512):
+        o = T.ff[:, 512 * t + j0:512 * t + j1]
+        i = T.nat[:, :].indirect(T.flist[:, 32 * t + j0 // 16:32 * t + j1 // 16])
+        w = [e_n["V"], e_n["S"], e_sel[t]]
+        e_f[t].append((j0, V(w, lambda: cp(o, i)) if q == "V" else act(w, o, i, F.Copy)))
+
+    e_pt, last = {}, [None]
+
+    def collect(k):
+        pe.wait_ge(T.sem["far%d" % k], len(eng) // len(groups[k]) * len(groups[k]))
+        for t in groups[k]:
+            last[0] = pe.matmul(p[5][0:64, 0:128], T.fland[:, 64 * senders[t]:64 * senders[t] + 64], T.ident[:, :], start=t == 0, stop=t == N - 2)
+
+    def sensors(t):
+        for c in range(4):
+            use("P", [e for j0, e in e_f[t] if j0 < 128 * c + 128] + [e_wd])
+            f = T.ff[:, 512 * t + 128 * c:512 * t + 128 * c + 128]
+            if t == N - 1:
+                use("P", [e_wf])
+                pe.matmul(p[5][0:64, 0:128], T.wf[:, 3 - c:67 - c], f, start=False, stop=False)
+            else:
+                o = 64 * at[t][1]
+                mm = pe.matmul(banks[at[t][0]][:, o + c:o + 64:4], f, T.wd[:, 16:32], start=True, stop=True)
+        if t < N - 1:
+            e_pt[t] = run("P", [], lambda: mm)
+
+    def send(k):
+        tts = groups[k]
+        e = V([e_pt[t] for t in tts], cp, T.fsend[:, 64 * tts[0]:64 * tts[-1] + 64], banks[k][:, 0:64 * len(tts)])
+        use("G", [e])
+        n = len(eng) // len(tts)
+        g.remote_dma_fused([RemoteDMATransfer(dst_ids=[dst_id(order[t])], dma_engine_mask=bits(eng[n * i:n * i + n]), remote_sem=T.sem["far%d" % k],
+                                              srcs=[T.fsend[:, 64 * t:64 * t + 64]], dsts=[T.fland[:, 64 * rank:64 * rank + 64]])
+                            for i, t in enumerate(tts)], local_sem=T.sem.fsent)
+
+    select(0)
+    gather("V", 0, 0, 256)
+    gather("S", 0, 256, 512)
+    sensors(0)
+    select(1)
+    gather("V", 1, 0, 256)
+    gather("S", 1, 256, 512)
+    send(0)
+    sensors(1)
+    gather("S", 2)
+    sensors(2)
+    gather("V", 3)
+    send(1)
+    sensors(3)
+    gather("S", 4)
+    sensors(4)
+    gather("V", 5, 0, 320)
+    send(2)
+    gather("S", 5, 320, 512)
+    sensors(5)
+    gather("V", 6, 0, 256)
+    gather("S", 6, 256, 512)
+    send(3)
+    sensors(6)
+    send(4)
+    gather("V", 7, 0, 128)
+    gather("S", 7, 128, 512)
+    e_w1 = chain([e_ac, e_idf, e_sel[0]], [lambda: pe.matmul(p[6][0:1, 0:16], ac, T.identf[0:16, 0:16], start=True, stop=True)])
+    collect(0)
+    collect(1)
+    sensors(7)
+    e_w2 = V([e_w1, e_wc], tt, T.w2[0:1, :], p[6][0:1, 0:16], T.wc[0:1, :], A.add)
+    e_w = run("Y", [e_w2], lambda: g.sync.dma_start(T.w[:, :], T.w2[0:1, :]), inc=16)
+
+    for k in range(2, len(groups)):
+        collect(k)
+    e_fin = run("P", [], lambda: last[0])
+    e_y = V([e_fin], cp, T.ysb[0:64, :], p[5][0:64, 0:128])
+    e_st = run("Y", [e_y], lambda: g.sync.dma_start(T.y[:, :], T.ysb[0:64, :]), inc=16)
+    use("Y", [e_w, e_st])
+    g.wait_ge(T.sem.ssent, len(eng))
+    g.wait_ge(T.sem.csent, len(eng))
+    g.wait_ge(T.sem.fsent, len(groups) * len(eng))
+    for e in events:
+        if not e["used"]:
+            g.wait_ge(e["sem"], e["total"])

@@ -2,20 +2,23 @@ from concourse.bass import DstId, RemoteDMATransfer
 from concourse.mybir import AluOpType as A, ActivationFunctionType as F
 
 _SB = {
-    "int32": "posi 2 taus 256 vi 128 e8s 128 pgi 2 wdi 16 wdm 16 pcol 2 rcol 2 r4 2 d2w 16 lo32 16 d2i 256 hi 256",
-    "uint16": "tauo 256 lo 16 nl 16 flist 256",
-    "bfloat16": "posf 2 trs 8192 nat 4096 e8 128 ones 256 ident 128 wd 144 wf 80 vc 256 cland 256 xq 16 lxa 128 lxb 128 em 256 "
-                "dga 256 dgb 256 ff 4096 fsend 448 fland 512",
-    "float32": "negp 2 lw 140 pgf 2 pf 2 rf 2 c16 2 c4 2 dyw 2 yy 256 xx 256 yrot 256 sy 256 t1 16 sw 16 "
-               "hm 256 prod 256 dg 64 dd 64 a3 32 a4 16 dy2 256 dy2s 256 dx2 2 dxs 2 rfree 128 le 32 identf 128 sq 32 "
-               "one64 64 pw 260 tauf 256 taut 256 run 16 lt 16 acol 2 wc 16 w2 16 ysb 128",
+    "int32": "posi 2 tz 256 vi 128 pgi 2 pcol 2 rcol 2 r4 2 r12 2 r8 2 p8 2 i16 16 d2w 16 lo32 16 d2i 256 hi 256",
+    "uint16": "tauo 256 lo 16 nl 16 flist 256 off1 16 off2 16",
+    "bfloat16": "posf 2 trs 8192 nat 4096 e8 128 ones 128 eights 256 ident 128 wd 144 wf 80 vc 256 cland 256 xq 16 em 256 dgm 64 "
+                "ff 4096 fsend 448 fland 512",
+    "float16": "lh 128",
+    "float32": "cbx 8 cby 2 bx 8 by 2 lw 140 pgf 2 rf 2 rh 2 c4 2 p8f 2 cv 2 yy 64 xx 64 yrot 256 sx 256 sqx 16 sqy 16 "
+               "hm 256 prod 256 seg 64 runq 64 dy2 256 dy2s 256 dx2 2 dxs 2 rfree 128 rf8 128 lxa 128 le 32 identf 128 sq 32 "
+               "one16 16 tp 256 tq 256 taut 256 run 24 lt 24 acol 2 wc 16 w2 16 ysb 128",
 }
 SCRATCH = {"p%d" % _k: ("psum", [128, 512], "float32") for _k in range(8)}
 for _d in _SB:
     _l = _SB[_d].split()
     for _k in range(0, len(_l), 2):
         SCRATCH[_l[_k]] = ("sbuf", [128, int(_l[_k + 1])], _d)
-SEMAPHORES = ["carr%d" % _k for _k in range(8)] + ["far%d" % _k for _k in range(5)] + ["csent", "fsent", "shared", "ssent"] + ["e%d" % _k for _k in range(130)]
+SEMAPHORES = ["carr%d" % _k for _k in range(8)] + ["far%d" % _k for _k in range(5)] + ["csent", "fsent", "shared", "ssent"] + ["e%d" % _k for _k in range(132)]
+
+NAT_V, NAT_S = [1792], [1920, 128, 256]
 
 
 def rank_program(g, core, T, topo):
@@ -64,7 +67,9 @@ def rank_program(g, core, T, topo):
     p = [T["p%d" % k] for k in range(8)]
 
     e_pos = run("Y", [], lambda: g.sync.dma_start(T.posi[0:8, :], T.pos[:, :]), inc=16)
-    e_tau = run("S", [], lambda: sca.dma_start(T.taus[:, :], T.tau[:, :]), inc=16)
+    e_tau = event()
+    for o in range(2):
+        run("SY"[o], [], lambda: (sca, g.sync)[o].dma_start(T.tz[:, 128 * o:128 * o + 128], T.tau[o:8:2, :]), ev=e_tau, inc=16)
     e_tr = run("Y", [], lambda: g.sync.dma_start(T.trs[:, :], T.tr[:, :]), inc=16)
 
     def kind(a, b):
@@ -101,72 +106,64 @@ def rank_program(g, core, T, topo):
     iota_i = lambda out, pat, base, cm: run("G", [], lambda: g.iota(out, pat, base, cm))
     iota_f = lambda out, pat, base, ev=None: run("G", [], lambda: g.iota(out, pat, base, 0, allow_small_or_imprecise_dtypes=True), ev=ev)
     sel = lambda waits, out, in_, pat, op, base, cm, ev=None: run("G", waits, lambda: g.affine_select(out, in_, pat, op, 0.0, base, cm), ev=ev)
-    e_one64 = V([], vec.memset, T.one64[:, :], 1.0)
     e_ones = V([], vec.memset, T.ones[:, :], 1.0)
-    e_wd0 = V([], vec.memset, T.wd[:, :], 0.0)
-    e_pw0 = V([], vec.memset, T.pw[:, :], 0.0)
-    e_tab0 = V([], vec.memset, T.wf[:, :] if rank < mate else T.le[:, :], 0.0)
+    e_fill = event()
+    V([], vec.memset, T.cby[:, :], 0.0, ev=e_fill)
+    V([], vec.memset, T.lw[:, 0:12], 0.0, ev=e_fill)
     e_pcol = iota_i(T.pcol[:, 0:1], [[1, 1]], 0, 1)
-    e_vi = iota_i(T.vi[:, :], [[1, 8], [16, 4], [0, 4]], 0, 0)
-    e_yy = iota_f(T.yy[:, :], [[0, 16], [16, 16]], 8)
-    e_xx = iota_f(T.xx[:, :], [[16, 16], [0, 16]], 8)
-    e_pw = event()
-    for o in range(2):
-        sel([e_one64, e_pw0], T.pw[:, 130 * o + 1:130 * o + 129:2], T.one64[:, :], [[-32, 4], [-1, 16]], A.is_equal, -16 * o, 1, ev=e_pw)
-    e_wdi = iota_i(T.wdi[:, :], [[1, 16]], 128, -1)
-    e_ident = sel([e_ones], T.ident[:, :], T.ones[:, 0:128], [[-1, 128]], A.is_equal, 0, 1)
+    e_i16 = iota_i(T.i16[:, :], [[16, 8], [128, 2]], 0, 0)
+    e_e8 = sel([e_ones], T.e8[0:8, :], T.ones[0:8, :], [[-1, 8], [0, 16]], A.is_equal, 0, 1)
+    e_yy = iota_f(T.yy[:, :], [[16, 16], [0, 4]], 8)
+    e_xx = iota_f(T.xx[:, :], [[0, 16], [16, 4]], 8)
+    e_vi = iota_i(T.vi[:, :], [[16, 8], [128, 4], [0, 4]], 0, 0)
+    e_ident = sel([e_ones], T.ident[:, :], T.ones[:, :], [[-1, 128]], A.is_equal, 0, 1)
 
-    e_r = V([e_pcol], ts, T.rcol[:, 0:1], T.pcol[:, 0:1], 15, None, A.bitwise_and)
-    e_pgi = V([], ts, T.pgi[:, 0:1], T.pcol[:, 0:1], 4, None, A.arith_shift_right)
-    e_pf = V([], cp, T.pf[:, 0:1], T.pcol[:, 0:1])
-    e_e8s = V([e_vi], ts, T.e8s[0:8, :], T.vi[0:8, :], 15, None, A.bitwise_and)
-    e_pgf = V([e_pgi], cp, T.pgf[:, 0:1], T.pgi[:, 0:1])
-    e_e8 = V([e_e8s, e_pf], ts, T.e8[0:8, :], T.e8s[0:8, :], T.pf[0:8, 0:1], -1.0, A.is_equal, A.mult)
-    e_c16 = V([e_r], ts, T.c16[:, 0:1], T.rcol[:, 0:1], 16.0, 8.0, A.mult, A.add)
+    e_bits = event()
+    V([e_pcol], ts, T.rcol[:, 0:1], T.pcol[:, 0:1], 15, None, A.bitwise_and, ev=e_bits)
+    V([], ts, T.r4[:, 0:1], T.pcol[:, 0:1], 3, None, A.bitwise_and, ev=e_bits)
+    V([], ts, T.r12[:, 0:1], T.pcol[:, 0:1], 12, None, A.bitwise_and, ev=e_bits)
+    V([], ts, T.r8[:, 0:1], T.pcol[:, 0:1], 7, None, A.bitwise_and, ev=e_bits)
+    V([], ts, T.p8[:, 0:1], T.pcol[:, 0:1], 3, 1, A.arith_shift_right, A.bitwise_and, ev=e_bits)
+    V([], ts, T.pgi[:, 0:1], T.pcol[:, 0:1], 112, None, A.bitwise_and, ev=e_bits)
+    e_cols = event()
+    V([e_bits], cp, T.rf[:, 0:1], T.rcol[:, 0:1], ev=e_cols)
+    V([], ts, T.cbx[:, 0:1], T.r4[:, 0:1], 16.0, -24.0, A.mult, A.add, ev=e_cols)
+    V([e_fill], ts, T.cby[:, 0:1], T.r12[:, 0:1], 4.0, -24.0, A.mult, A.add, ev=e_cols)
+    V([], ts, T.p8f[:, 0:1], T.p8[:, 0:1], -1.0, None, A.add, ev=e_cols)
+    V([], cp, T.pgf[:, 0:1], T.pgi[:, 0:1], ev=e_cols)
+    e_off1 = V([e_cols, e_i16], ts, T.off1[:, :], T.i16[:, :], T.rf[:, 0:1], None, A.add)
+    e_cv = V([], ts, T.cv[:, 0:1], T.r8[:, 0:1], 32.0, T.p8f[:, 0:1], A.mult, A.add)
+    e_cbq = V([e_yy], ts, T.cbx[:, 1:5], T.yy[:, 0:16:4], 4.0, -32.0, A.mult, A.add)
+
+    e_tp = act([e_tau, e_off1], T.tp[:, :], T.tz[:, :].indirect(T.off1[:, :]), F.Copy)
 
     e_posf = V([e_pos], cp, T.posf[0:8, :], T.posi[0:8, :])
     e_pb = run("P", [e_e8, e_posf], lambda: pe.matmul(p[0][:, 0:2], T.e8[0:8, :], T.posf[0:8, :], start=True, stop=True))
-    e_rf = V([e_r], cp, T.rf[:, 0:1], T.rcol[:, 0:1])
-    e_xq = V([e_posf, e_ones], ts, T.xq[0:8, :], T.ones[0:8, 0:16], T.posf[0:8, 0:1], None, A.mult)
-    e_np = V([e_pb], cp, T.negp[:, :], p[0][:, 0:2])
-    nx, ny = T.negp[:, 0:1], T.negp[:, 1:2]
-    e_dyw = act([e_c16, e_np], T.dyw[:, 0:1], T.c16[:, 0:1], F.Square, bias=ny)
-    e_sy = act([e_yy], T.sy[:, :], T.yy[:, :], F.Square, bias=ny)
-    e_sx = act([e_xx], p[6][:, 0:256], T.xx[:, :], F.Square, bias=nx)
-    e_pq = run("P", [e_xq], lambda: pe.matmul(p[7][0:16, 0:128], T.xq[0:8, :], T.e8[0:8, :], start=True, stop=True))
+    e_off2 = V([e_cv], ts, T.off2[:, :], T.yy[:, 0:64:4], 0.125, T.cv[:, 0:1], A.mult, A.add)
+    e_by = V([e_pb], ts, T.by[:, :], T.cby[:, :], p[0][:, 1:2], None, A.subtract)
+    e_bx = V([e_cbq], ts, T.bx[:, 0:5], T.cbx[:, 0:5], p[0][:, 0:1], None, A.subtract)
+    ny = T.by[:, 1:2]
+    e_sy = act([e_by, e_yy], p[1][:, 0:64], T.yy[:, :], F.Square, bias=ny)
+    e_sx = [act([e_bx, e_xx], T.sx[:, 64 * q:64 * q + 64], T.xx[:, :], F.Square, bias=T.bx[:, 1 + q:2 + q]) for q in range(2)]
+    e_sqw = event()
+    act([], T.sqx[:, :], T.yy[:, 0:16], F.Square, ev=e_sqw, bias=T.bx[:, 0:1], scale=4.0)
+    act([], T.sqy[:, :], T.xx[:, 0:16], F.Square, ev=e_sqw, bias=T.by[:, 0:1], scale=4.0)
+    e_sx += [act([], T.sx[:, 64 * q:64 * q + 64], T.xx[:, :], F.Square, bias=T.bx[:, 1 + q:2 + q]) for q in range(2, 4)]
 
-    e_t1 = V([e_yy, e_np], ts, T.t1[:, :], T.yy[:, 0:16], nx, None, A.add)
-    e_l = event()
-    V([], vec.memset, T.lw[:, 0:12], 0.0, ev=e_l)
-    e_sw = V([e_t1], tt, T.sw[:, :], T.t1[:, :], T.t1[:, :], A.mult)
-    V([e_vi, e_pgf], ts, T.lw[:, 12:140], T.vi[:, :], T.pgf[:, 0:1], None, A.is_equal, ev=e_l)
-    e_d2w = V([e_sw, e_dyw], ts, T.d2w[:, :], T.sw[:, :], T.dyw[:, 0:1], None, A.add)
-
-    e_tauf = V([e_tau], cp, T.tauf[:, :], T.taus[:, :])
-
-    def pairs(o):
-        use("P", [e_tauf, e_pw])
-        for x in range(2):
-            mm = pe.matmul(p[5][:, 128 * o:128 * o + 128], T.pw[:, 130 * o + 1 - x:130 * o + 129 - x], T.tauf[:, 128 * x:128 * x + 128],
-                           start=x == 0, stop=x == 1)
-        return run("P", [], lambda: mm)
-
-    pairs(0)
-    e_lo32 = V([e_d2w], ts, T.lo32[:, :], T.d2w[:, :], 5, 255, A.arith_shift_right, A.bitwise_and)
-    e_lo = V([e_lo32], cp, T.lo[:, :], T.lo32[:, :])
-    e_wdm = V([e_wdi], ts, T.wdm[:, :], T.wdi[:, :], 15, None, A.bitwise_and)
-    e_d2i = V([e_sx, e_sy], tt, T.d2i[:, :], p[6][:, 0:256], T.sy[:, :], A.add)
-    e_hi = V([e_d2i], ts, T.hi[:, :], T.d2i[:, :], 13, None, A.arith_shift_right)
-
+    e_zero = event()
+    V([], vec.memset, T.wf[:, :] if rank < mate else T.le[:, :], 0.0, ev=e_zero)
+    V([], ts, T.rh[:, 0:1], T.rcol[:, 0:1], 0.5, None, A.add, ev=e_zero)
+    V([], ts, T.c4[:, 0:1], T.r4[:, 0:1], 16.0, 8.0, A.mult, A.add, ev=e_zero)
     e_shared = {"n": len(events), "sem": T.sem.shared, "total": len(eng), "knows": set(), "used": False}
     events.append(e_shared)
+    picks = lambda waits, out: V(waits, ts, out, T.yy[:, 0:64:4], 1.0 / 16, T.rh[:, 0:1], A.mult, A.is_equal)
     if rank < mate:
-        e_made = V([e_wdm, e_tab0], ts, T.wf[:, 3:67:4], T.wdm[:, :], 0.0, None, A.is_equal)
+        e_made = picks([e_zero], T.wf[:, 3:67:4])
         e_wf, e_le, table = e_made, e_shared, T.wf
     else:
         e_made = event()
         for h in range(2):
-            sel([e_l, e_tab0], T.le[:, 17 * h:17 * h + 15:2], T.lw[:, 12:140:16], [[0, 8]], A.is_equal, 0, 0, ev=e_made)
+            V([e_zero], ts, T.le[:, 17 * h:17 * h + 15:2], T.yy[:, 0:32:4], T.pgf[:, 0:1], 8.0, A.subtract, A.is_equal, ev=e_made)
         e_wf, e_le, table = e_shared, e_made, T.le
     use("G", [e_made])
     g.remote_dma_fused([RemoteDMATransfer(dst_ids=[dst_id(mate)], dma_engine_mask=bits(eng), remote_sem=T.sem.shared,
@@ -174,90 +171,110 @@ def rank_program(g, core, T, topo):
     e_yrot = event()
     for t, q, d, n in runs:
         iota_f(T.yrot[:, 32 * t:32 * t + 32 * n], [[32 * d, n], [1, 32]], 32 * q, ev=e_yrot)
-    e_rfree = iota_f(T.rfree[0:16, :], [[0, 8], [1, 16]], 0)
+    e_rfree = iota_f(T.rfree[0:16, :], [[0, 8], [1, 16]], 128)
 
-    e_hm = V([e_hi, e_rf], ts, T.hm[:, :], T.hi[:, :], T.rf[:, 0:1], None, A.is_equal)
-    e_prod = [V([e_hm, e_lo, e_tau], lambda k=k: tt(T.prod[:, 128 * k:128 * k + 128], T.taus[:, :].indirect(T.lo[:, 8 * k:8 * k + 8]),
-                                                    T.hm[:, 128 * k:128 * k + 128], A.mult)) for k in range(2)]
+    e_dgm = V([e_zero, e_xx], ts, T.dgm[:, :], T.xx[:, :], T.c4[:, 0:1], -16384.0, A.not_equal, A.mult)
+    e_l = V([e_vi], ts, T.lw[:, 12:140], T.vi[:, :], T.pgf[:, 0:1], None, A.is_equal)
+    e_tq = V([e_tp], vec.transpose, T.tq[:, :], T.tp[:, :])
+    e_taut = act([e_tq, e_off2], T.taut[:, :], T.tq[:, :].indirect(T.off2[:, :]), F.Copy)
+
+    d2i = lambda q: V([e_sy, e_sx[q]], tt, T.d2i[:, 64 * q:64 * q + 64], p[1][:, 0:64], T.sx[:, 64 * q:64 * q + 64], A.add)
+    half = lambda buf, k: buf[:, 128 * k:128 * k + 128]
+    hi = lambda k: V(e_d2i[2 * k:2 * k + 2], ts, half(T.hi, k), half(T.d2i, k), 5, 15, A.arith_shift_right, A.bitwise_and)
+    hm = lambda k: V([e_hi[k]], ts, half(T.hm, k), half(T.hi, k), T.rf[:, 0:1], None, A.is_equal)
+    e_d2i = [d2i(0), d2i(1)]
+    e_d2w = V([e_sqw], tt, T.d2w[:, :], T.sqx[:, :], T.sqy[:, :], A.add)
+    e_hi = [hi(0)]
+    e_lo32 = V([e_d2w], ts, T.lo32[:, :], T.d2w[:, :], 9, None, A.arith_shift_right)
+    e_d2i += [d2i(2), d2i(3)]
+    e_hm = [hm(0)]
+    e_lo = V([e_lo32], cp, T.lo[:, :], T.lo32[:, :])
+    e_hi.append(hi(1))
+    prod = lambda k: V([e_hm[k], e_lo, e_taut], tt, half(T.prod, k), T.taut[:, :].indirect(T.lo[:, 8 * k:8 * k + 8]), half(T.hm, k), A.mult)
+    e_prod = [prod(0)]
+    e_hm.append(hm(1))
+    e_prod.append(prod(1))
+    e_seg = V([], ts, T.seg[:, :], T.xx[:, :], 8.0, None, A.not_equal)
+    e_wd0 = V([], vec.memset, T.wd[:, :], 0.0)
+    e_tauo = V([], cp, T.tauo[:, :], T.taut[:, :])
+    e_wd = picks([e_wd0], T.wd[:, 16:32])
+    use("P", [e_dgm, e_ident])
+    pe.matmul(p[2][:, 0:64], T.ident[:, :], T.dgm[:, :], start=True, stop=False)
     for q in range(4):
         use("P", [e_prod[q // 2], e_l])
-        mm = pe.matmul(p[1][:, 0:64], T.lw[:, 12 - 4 * q:140 - 4 * q], T.prod[:, 64 * q:64 * q + 64], start=q == 0, stop=q == 3)
+        mm = pe.matmul(p[2][:, 0:64], T.lw[:, 12 - 4 * q:140 - 4 * q], T.prod[:, 64 * q:64 * q + 64], start=False, stop=q == 3)
     e_s = run("P", [], lambda: mm)
-    e_z = pairs(1)
+    e_more = event()
+    V([], ts, T.xq[0:8, :], T.ones[0:8, 0:16], T.posf[0:8, 0:1], 0.125, A.mult, A.mult, ev=e_more)
+    V([], vec.memset, T.eights[0:16, :], 8.0, ev=e_more)
+    V([], vec.memset, T.one16[0:16, :], 1.0, ev=e_more)
+    V([], vec.memset, T.run[0:16, 16:24], 3.0e7, ev=e_more)
+    e_runq = V([e_s, e_seg], vec.tensor_tensor_scan, T.runq[:, :], T.seg[:, :], p[2][:, 0:64], 0.0, A.mult, A.max)
+    e_nl = V([e_runq], cp, T.nl[:, :], T.runq[:, 3:64:4])
 
-    e_dx2 = act([e_rf], T.dx2[:, 0:1], T.rf[:, 0:1], F.Square, bias=nx)
-    e_dxs = act([e_dx2], T.dxs[:, 0:1], T.dx2[:, 0:1], F.Copy, bias=-15.5 / 32, scale=1.0 / 32)
+    e_dx2 = act([], T.dx2[:, 0:1], T.rf[:, 0:1], F.Square, bias=T.bx[:, 3:4])
     e_idf = act([e_ident], T.identf[:, :], T.ident[:, :], F.Copy)
+    e_dxs = act([e_dx2], T.dxs[:, 0:1], T.dx2[:, 0:1], F.Copy, bias=-15.5 / 32, scale=1.0 / 32)
     e_dy2 = act([e_yrot], T.dy2[:, :], T.yrot[:, :], F.Square, bias=ny)
     e_dy2s = act([e_dxs, e_dy2], T.dy2s[:, :], T.dy2[:, :], F.Identity, bias=T.dxs[:, 0:1], scale=1.0 / 32)
-    e_r4 = V([], ts, T.r4[:, 0:1], T.pcol[:, 0:1], 3, None, A.bitwise_and)
-    e_wd = V([e_wdm, e_wd0], ts, T.wd[:, 16:32], T.wdm[:, :], 0.0, None, A.is_equal)
-    e_c4 = V([e_r4], ts, T.c4[:, 0:1], T.r4[:, 0:1], 16.0, 8.0, A.mult, A.add)
-    e_dg = V([e_xx, e_c4], ts, T.dg[:, :], T.xx[:, 0:64], T.c4[:, 0:1], None, A.is_equal)
-    e_dd = V([e_s, e_dg], tt, T.dd[:, :], p[1][:, 0:64], T.dg[:, :], A.mult)
-    e_a3 = V([e_dd], tt, T.a3[:, :], T.dd[:, 0:32], T.dd[:, 32:64], A.add)
-    e_a4 = V([e_a3], tt, T.a4[:, :], T.a3[:, 0:16], T.a3[:, 16:32], A.add)
-    e_nl = V([e_a4], cp, T.nl[:, :], T.a4[:, :])
-
-    e_tt, e_tauo = event(), [None, None]
-    for k in range(8):
-        V([e_z], vec.transpose, T.taut[:, 32 * k:32 * k + 32], p[5][:, k:256:8], ev=e_tt)
-    for k in range(2):
-        e_tauo[k] = V([e_tt], cp, T.tauo[:, 128 * k:128 * k + 128], T.taut[:, 128 * k:128 * k + 128])
+    parts = [(0, 64), (64, 256)]
+    e_rf8 = act([e_rfree], T.rf8[0:16, :], T.rfree[0:16, :], F.Copy, scale=0.125)
+    e_pq = run("P", [e_more], lambda: pe.matmul(p[4][0:16, 0:128], T.xq[0:8, :], T.e8[0:8, :], start=True, stop=True))
 
     e_va = [act([e_tr, e_nl], T.vc[:, 64 * k:64 * k + 64], T.trs[:, :].indirect(T.nl[:, 4 * k:4 * k + 4]), F.Copy) for k in (0, 1)]
     e_vv = [V([e_tr, e_nl], cp, T.vc[:, 64 * k:64 * k + 64], T.trs[:, :].indirect(T.nl[:, 4 * k:4 * k + 4])) for k in (2, 3)]
-    e_lxa = V([e_pq, e_rfree], tt, T.lxa[0:16, :], p[7][0:16, 0:128], T.rfree[0:16, :], A.add)
-    e_lxb = V([], vec.memset, T.lxb[0:16, :], 8.0)
+    e_lxa = V([e_pq, e_rf8], tt, T.lxa[0:16, :], T.rf8[0:16, :], p[4][0:16, 0:128], A.subtract)
     use("P", [e_wd])
     for k in (0, 1, 4, 5, 2, 3, 6, 7):
         use("P", [(e_va + e_vv)[k // 2]])
         o = 32 * (k // 2)
-        mm = pe.matmul(p[2][o:o + 32, 0:32], T.wd[:, 16 - 16 * (k % 2):48 - 16 * (k % 2)], T.vc[:, 32 * k:32 * k + 32], start=k % 2 == 0, stop=k % 2 == 1)
+        mm = pe.matmul(p[3][o:o + 32, 0:32], T.wd[:, 16 - 16 * (k % 2):48 - 16 * (k % 2)], T.vc[:, 32 * k:32 * k + 32], start=k % 2 == 0, stop=k % 2 == 1)
     e_cs = run("P", [], lambda: mm)
     own = slice(32 * rank, 32 * rank + 32)
-    e_own = V([e_cs], cp, T.cland[:, own], p[2][:, 0:32])
+    e_own = V([e_cs], cp, T.cland[:, own], p[3][:, 0:32])
     use("G", [e_own])
     g.remote_dma_fused([RemoteDMATransfer(dst_ids=[dst_id(q) for q in others], dma_engine_mask=bits(eng), remote_sem=T.sem["carr%d" % rank],
                                           srcs=[T.cland[:, own]], dsts=[T.cland[:, own] for q in others])], local_sem=T.sem.csent)
     e_em = event()
     for t, q, d, n in runs:
-        sel([e_ones], T.em[0:16, 32 * t:32 * t + 32 * n], T.ones[0:16, 0:32 * n], [[-2 * d, n], [-1, 2], [0, 16]], A.is_equal, -2 * q, 1, ev=e_em)
-    e_wc = iota_f(T.wc[0:1, :], [[16, 16]], 0)
+        sel([e_more], T.em[0:16, 32 * t:32 * t + 32 * n], T.eights[0:16, 0:32 * n], [[-2 * d, n], [-1, 2], [0, 16]], A.is_equal, -2 * q, 1, ev=e_em)
+    e_wc = iota_f(T.wc[0:1, :], [[16, 16]], 8)
 
-    e_n = {q: event() for q in "VS"}
-    for k in range(8):
-        q = "VS"[k // 4]
-        o, i = T.nat[:, k:4096:8], T.trs[:, :].indirect(T.tauo[:, 32 * k:32 * k + 32])
+    e_n, at_n = {q: event() for q in "VS"}, [0]
+
+    def nat(q, n):
+        j = at_n[0]
+        at_n[0] += n
+        o, i = T.nat[:, j:j + n], T.trs[:, :].indirect(T.tauo[:, j // 16:(j + n) // 16])
         if q == "V":
-            V([e_tr, e_tauo[0]], cp, o, i, ev=e_n[q])
+            V([e_tr, e_tauo], cp, o, i, ev=e_n[q])
         else:
-            act([e_tr, e_tauo[1]], o, i, F.Copy, ev=e_n[q])
+            act([e_tr, e_tauo], o, i, F.Copy, ev=e_n[q])
 
-    use("P", [e_own, e_ident])
-    pe.matmul(p[3][:, 0:32], T.ident[:, :], T.cland[:, own], start=True, stop=False)
-    parts = [(0, 64), (64, 256)]
-    use("P", [e_idf, e_dy2s, e_lxa])
+    for n in NAT_V:
+        nat("V", n)
+    nat("S", NAT_S[0])
+
+    use("P", [e_own])
+    pe.matmul(p[5][:, 0:32], T.ident[:, :], T.cland[:, own], start=True, stop=False)
+    use("P", [e_idf, e_dy2s])
     for k, (c0, c1) in enumerate(parts):
         pe.matmul(p[6 + k][:, 0:c1 - c0], T.identf[:, :], T.dy2s[:, c0:c1], start=True, stop=False)
     for q in senders[:-1]:
         pe.wait_ge(T.sem["carr%d" % q], len(eng))
-        mm = pe.matmul(p[3][:, 0:32], T.ident[:, :], T.cland[:, 32 * q:32 * q + 32], start=False, stop=q == senders[N - 2])
+        mm = pe.matmul(p[5][:, 0:32], T.ident[:, :], T.cland[:, 32 * q:32 * q + 32], start=False, stop=q == senders[N - 2])
     e_tot = run("P", [], lambda: mm)
-    e_sq = act([e_tot], T.sq[:, :], p[3][:, 0:32], F.Square)
-    e_e = chain([e_sq, e_le], [lambda: pe.matmul(p[4][0:16, 0:16], T.le[:, 0:16], T.sq[:, 0:16], start=True, stop=False),
-                               lambda: pe.matmul(p[4][0:16, 0:16], T.le[:, 16:32], T.sq[:, 16:32], start=False, stop=True)])
-    e_run = V([e_e, e_one64], vec.tensor_tensor_scan, T.run[0:16, :], T.one64[0:16, 0:16], p[4][0:16, 0:16], 0.0, A.mult, A.max)
+    e_sq = act([e_tot], T.sq[:, :], p[5][:, 0:32], F.Square)
+    nat("S", NAT_S[1])
+    e_e = chain([e_sq, e_le, e_lxa], [lambda: pe.matmul(p[4][0:16, 0:16], T.le[:, 0:16], T.sq[:, 0:16], start=True, stop=False),
+                                      lambda: pe.matmul(p[4][0:16, 0:16], T.le[:, 16:32], T.sq[:, 16:32], start=False, stop=True)])
+    e_run = V([e_e, e_more], vec.tensor_tensor_scan, T.run[0:16, 0:16], T.one16[0:16, :], p[4][0:16, 0:16], 0.0, A.mult, A.max)
     ac = T.acol[0:16, 0:1]
     e_ac = act([e_run], T.lt[0:16, :], T.run[0:16, :], F.Sign, bias=T.run[0:16, 15:16], scale=-1.0, accum_out=ac)
-    e_d = []
-    for k, (c0, c1) in enumerate(parts):
-        e_a = V([e_ac, e_em], ts, T.dga[0:16, c0:c1], T.em[0:16, c0:c1], ac, None, A.mult)
-        e_b = act([e_ac, e_em], T.dgb[0:16, c0:c1], T.em[0:16, c0:c1], F.Square, scale=ac)
-        o = p[6 + k][:, 0:c1 - c0]
-        use("P", [e_a])
-        pe.matmul(o, T.lxa[0:16, :], T.dga[0:16, c0:c1], start=False, stop=False)
-        e_d.append(chain([e_b, e_lxb], [lambda: pe.matmul(o, T.lxb[0:16, :], T.dgb[0:16, c0:c1], start=False, stop=True)]))
+    nat("S", NAT_S[2])
+    e_lh = V([e_ac, e_lxa], ts, T.lh[0:16, :], T.lxa[0:16, :], ac, ac, A.add, A.mult)
+    e_d = [chain([e_lh, e_em], [lambda: pe.matmul(p[6 + k][:, 0:c1 - c0], T.lh[0:16, :], T.em[0:16, c0:c1], start=False, stop=True)])
+           for k, (c0, c1) in enumerate(parts)]
 
     e_sel = {}
 

@@ -2,23 +2,27 @@ from concourse.bass import DstId, RemoteDMATransfer
 from concourse.mybir import AluOpType as A, ActivationFunctionType as F
 
 _SB = {
-    "int32": "posi 2 tz 256 vi 128 pgi 2 pcol 2 rcol 2 r4 2 r12 2 r8 2 p8 2 i16 16 d2w 16 lo32 16 d2i 256 hi 256",
-    "uint16": "tauo 256 lo 16 nl 16 flist 256 off1 16 off2 16",
-    "bfloat16": "posf 2 trs 8192 nat 4096 e8 128 ones 128 eights 256 ident 128 wd 144 wf 80 vc 256 cland 256 xq 16 em 256 dgm 64 "
+    "int32": "posi 16 posb 16 tz 256 vi 128 pgi 2 pg2 2 pcol 2 rcol 2 r4 2 r12 2 i16 16 d2w 16 lo32 16 hi32 16",
+    "uint16": "tauo 256 lo 16 hi 16 nl 16 flist 256 off1 16 off2 16 offp 2",
+    "bfloat16": "trs 8192 nat 4096 ones 128 eights 32 ident 128 wd 160 wf 80 vc 256 cland 256 xq 16 lxa 128 em 256 dgm 64 hm 256 "
                 "ff 4096 fsend 448 fland 512",
     "float16": "lh 128",
-    "float32": "cbx 8 cby 2 bx 8 by 2 lw 140 pgf 2 rf 2 rh 2 c4 2 p8f 2 cv 2 yy 64 xx 64 yrot 256 sx 256 sqx 16 sqy 16 "
-               "hm 256 prod 256 seg 64 runq 64 dy2 256 dy2s 256 dx2 2 dxs 2 rfree 128 rf8 128 lxa 128 le 32 identf 128 sq 32 "
-               "one16 16 tp 256 tq 256 taut 256 run 24 lt 24 acol 2 wc 16 w2 16 ysb 128",
+    "float32": "negp 32 lw 140 pgf 2 rf 2 r8 2 r128 2 c4 2 c12 2 cv 2 yy 64 xx 64 xyw 32 dxy 32 sqw 32 yb 32 byq 8 "
+               "prod 256 dg 64 seg 64 runq 64 dy2 256 dy2s 256 dxc 2 dx2 2 dxs 2 le 32 identf 128 sq 32 "
+               "one16 16 tp 256 tq 256 taut 256 run 24 lt 24 acol 2 wc 16 w2 16 ysb 64",
 }
 SCRATCH = {"p%d" % _k: ("psum", [128, 512], "float32") for _k in range(8)}
 for _d in _SB:
     _l = _SB[_d].split()
     for _k in range(0, len(_l), 2):
         SCRATCH[_l[_k]] = ("sbuf", [128, int(_l[_k + 1])], _d)
-SEMAPHORES = ["carr%d" % _k for _k in range(8)] + ["far%d" % _k for _k in range(5)] + ["csent", "fsent", "shared", "ssent"] + ["e%d" % _k for _k in range(132)]
+SEMAPHORES = ["carr%d" % _k for _k in range(8)] + ["far%d" % _k for _k in range(7)] + ["csent", "fsent", "shared", "ssent"] + ["e%d" % _k for _k in range(130)]
 
-NAT_V, NAT_S = [1792], [1920, 128, 256]
+NAT_V, NAT_S = [128, 1600, 96, 160], [0, 1664, 160, 288]
+GROUPS = [[0], [1, 2], [3, 4], [5], [6]]
+PLAN = ["lists", ("V", 0, 256), ("S", 256, 544), ("V", 544, 896), ("V", 0), ("S", 896, 1536), ("V", 1536, 2048), ("V", 1),
+        ("S", 2048, 2560), ("V", 2560, 2816), ("S", 2816, 3072), ("V", 3072, 3264), ("V", 2), ("S", 3264, 3392), ("V", 3392, 3488), ("V", 3),
+        ("S", 3488, 3584), ("V", 3584, 3744), ("V", 4), ("S", 3744, 4096)]
 
 
 def rank_program(g, core, T, topo):
@@ -66,7 +70,7 @@ def rank_program(g, core, T, topo):
 
     p = [T["p%d" % k] for k in range(8)]
 
-    e_pos = run("Y", [], lambda: g.sync.dma_start(T.posi[0:8, :], T.pos[:, :]), inc=16)
+    e_pos = run("Y", [], lambda: g.sync.dma_start(T.posi[0:1, :], T.pos[:, :]), inc=16)
     e_tau = event()
     for o in range(2):
         run("SY"[o], [], lambda: (sca, g.sync)[o].dma_start(T.tz[:, 128 * o:128 * o + 128], T.tau[o:8:2, :]), ev=e_tau, inc=16)
@@ -95,136 +99,131 @@ def rank_program(g, core, T, topo):
 
     eng = [e for e in topo.engines(core, T.cores[mate]) if all(e in topo.engines(core, T.cores[q]) for q in others)]
 
-    runs, t = [], 0
-    while t < N:
-        n, d = 1, (order[t + 1] - order[t] if t + 1 < N else 1)
-        while t + n < N and order[t + n] == order[t] + n * d:
-            n += 1
-        runs.append((t, order[t], d, n))
-        t += n
-
     iota_i = lambda out, pat, base, cm: run("G", [], lambda: g.iota(out, pat, base, cm))
     iota_f = lambda out, pat, base, ev=None: run("G", [], lambda: g.iota(out, pat, base, 0, allow_small_or_imprecise_dtypes=True), ev=ev)
     sel = lambda waits, out, in_, pat, op, base, cm, ev=None: run("G", waits, lambda: g.affine_select(out, in_, pat, op, 0.0, base, cm), ev=ev)
-    e_ones = V([], vec.memset, T.ones[:, :], 1.0)
     e_fill = event()
-    V([], vec.memset, T.cby[:, :], 0.0, ev=e_fill)
+    V([], vec.memset, T.wd[:, :], 0.0, ev=e_fill)
     V([], vec.memset, T.lw[:, 0:12], 0.0, ev=e_fill)
     e_pcol = iota_i(T.pcol[:, 0:1], [[1, 1]], 0, 1)
     e_i16 = iota_i(T.i16[:, :], [[16, 8], [128, 2]], 0, 0)
-    e_e8 = sel([e_ones], T.e8[0:8, :], T.ones[0:8, :], [[-1, 8], [0, 16]], A.is_equal, 0, 1)
-    e_yy = iota_f(T.yy[:, :], [[16, 16], [0, 4]], 8)
+    e_yy = iota_f(T.yy[:, :], [[16, 16], [0, 4]], 0)
     e_xx = iota_f(T.xx[:, :], [[0, 16], [16, 4]], 8)
+    e_posb = run("G", [e_pos], lambda: g.partition_broadcast(T.posb[:, :], T.posi[0:1, :], 128))
     e_vi = iota_i(T.vi[:, :], [[16, 8], [128, 4], [0, 4]], 0, 0)
-    e_ident = sel([e_ones], T.ident[:, :], T.ones[:, :], [[-1, 128]], A.is_equal, 0, 1)
 
     e_bits = event()
     V([e_pcol], ts, T.rcol[:, 0:1], T.pcol[:, 0:1], 15, None, A.bitwise_and, ev=e_bits)
     V([], ts, T.r4[:, 0:1], T.pcol[:, 0:1], 3, None, A.bitwise_and, ev=e_bits)
     V([], ts, T.r12[:, 0:1], T.pcol[:, 0:1], 12, None, A.bitwise_and, ev=e_bits)
-    V([], ts, T.r8[:, 0:1], T.pcol[:, 0:1], 7, None, A.bitwise_and, ev=e_bits)
-    V([], ts, T.p8[:, 0:1], T.pcol[:, 0:1], 3, 1, A.arith_shift_right, A.bitwise_and, ev=e_bits)
-    V([], ts, T.pgi[:, 0:1], T.pcol[:, 0:1], 112, None, A.bitwise_and, ev=e_bits)
+    V([], ts, T.pg2[:, 0:1], T.pcol[:, 0:1], 3, 14, A.arith_shift_right, A.bitwise_and, ev=e_bits)
+    e_ones = V([], vec.memset, T.ones[:, :], 1.0)
+    V([], vec.memset, T.wf[:, :] if rank < mate else T.le[:, :], 0.0, ev=e_fill)
     e_cols = event()
     V([e_bits], cp, T.rf[:, 0:1], T.rcol[:, 0:1], ev=e_cols)
-    V([], ts, T.cbx[:, 0:1], T.r4[:, 0:1], 16.0, -24.0, A.mult, A.add, ev=e_cols)
-    V([e_fill], ts, T.cby[:, 0:1], T.r12[:, 0:1], 4.0, -24.0, A.mult, A.add, ev=e_cols)
-    V([], ts, T.p8f[:, 0:1], T.p8[:, 0:1], -1.0, None, A.add, ev=e_cols)
-    V([], cp, T.pgf[:, 0:1], T.pgi[:, 0:1], ev=e_cols)
+    V([], ts, T.c4[:, 0:1], T.r4[:, 0:1], 16.0, 8.0, A.mult, A.add, ev=e_cols)
+    V([], ts, T.c12[:, 0:1], T.r12[:, 0:1], 4.0, -24.0, A.mult, A.add, ev=e_cols)
+    V([], ts, T.r8[:, 0:1], T.rcol[:, 0:1], 8.0, -255.0, A.is_ge, A.mult, ev=e_cols)
+    e_col2 = event()
+    for o in range(2):
+        V([], ts, T.offp[:, o:o + 1], T.pg2[:, 0:1], float(o), None, A.add, ev=e_col2)
+    V([], ts, T.pgf[:, 0:1], T.pg2[:, 0:1], 8.0, None, A.mult, ev=e_col2)
     e_off1 = V([e_cols, e_i16], ts, T.off1[:, :], T.i16[:, :], T.rf[:, 0:1], None, A.add)
-    e_cv = V([], ts, T.cv[:, 0:1], T.r8[:, 0:1], 32.0, T.p8f[:, 0:1], A.mult, A.add)
-    e_cbq = V([e_yy], ts, T.cbx[:, 1:5], T.yy[:, 0:16:4], 4.0, -32.0, A.mult, A.add)
+    e_ident = sel([e_ones], T.ident[:, :], T.ones[:, :], [[-1, 128]], A.is_equal, 0, 1)
+    picks = lambda waits, out: V(waits, ts, out, T.yy[:, 0:64:4], 1.0 / 16, T.rf[:, 0:1], A.mult, A.is_equal)
+    e_wd = picks([e_fill, e_yy], T.wd[:, 16:32])
+    e_xyw = event()
+    act([e_cols, e_yy], T.xyw[:, 0:16], T.yy[:, 0:16], F.Identity, ev=e_xyw, bias=T.c4[:, 0:1], scale=4.0)
+    act([e_xx], T.xyw[:, 16:32], T.xx[:, 0:16], F.Identity, ev=e_xyw, bias=T.c12[:, 0:1], scale=4.0)
+    e_cv = act([], T.cv[:, 0:1], T.rf[:, 0:1], F.Identity, bias=T.r8[:, 0:1], scale=32.0)
 
-    e_tp = act([e_tau, e_off1], T.tp[:, :], T.tz[:, :].indirect(T.off1[:, :]), F.Copy)
+    e_tp = [act([e_tau, e_off1], T.tp[:, 128 * k:128 * k + 128], T.tz[:, :].indirect(T.off1[:, 8 * k:8 * k + 8]), F.Copy) for k in range(2)]
 
-    e_posf = V([e_pos], cp, T.posf[0:8, :], T.posi[0:8, :])
-    e_pb = run("P", [e_e8, e_posf], lambda: pe.matmul(p[0][:, 0:2], T.e8[0:8, :], T.posf[0:8, :], start=True, stop=True))
-    e_off2 = V([e_cv], ts, T.off2[:, :], T.yy[:, 0:64:4], 0.125, T.cv[:, 0:1], A.mult, A.add)
-    e_by = V([e_pb], ts, T.by[:, :], T.cby[:, :], p[0][:, 1:2], None, A.subtract)
-    e_bx = V([e_cbq], ts, T.bx[:, 0:5], T.cbx[:, 0:5], p[0][:, 0:1], None, A.subtract)
-    ny = T.by[:, 1:2]
-    e_sy = act([e_by, e_yy], p[1][:, 0:64], T.yy[:, :], F.Square, bias=ny)
-    e_sx = [act([e_bx, e_xx], T.sx[:, 64 * q:64 * q + 64], T.xx[:, :], F.Square, bias=T.bx[:, 1 + q:2 + q]) for q in range(2)]
-    e_sqw = event()
-    act([], T.sqx[:, :], T.yy[:, 0:16], F.Square, ev=e_sqw, bias=T.bx[:, 0:1], scale=4.0)
-    act([], T.sqy[:, :], T.xx[:, 0:16], F.Square, ev=e_sqw, bias=T.by[:, 0:1], scale=4.0)
-    e_sx += [act([], T.sx[:, 64 * q:64 * q + 64], T.xx[:, :], F.Square, bias=T.bx[:, 1 + q:2 + q]) for q in range(2, 4)]
-
-    e_zero = event()
-    V([], vec.memset, T.wf[:, :] if rank < mate else T.le[:, :], 0.0, ev=e_zero)
-    V([], ts, T.rh[:, 0:1], T.rcol[:, 0:1], 0.5, None, A.add, ev=e_zero)
-    V([], ts, T.c4[:, 0:1], T.r4[:, 0:1], 16.0, 8.0, A.mult, A.add, ev=e_zero)
     e_shared = {"n": len(events), "sem": T.sem.shared, "total": len(eng), "knows": set(), "used": False}
     events.append(e_shared)
-    picks = lambda waits, out: V(waits, ts, out, T.yy[:, 0:64:4], 1.0 / 16, T.rh[:, 0:1], A.mult, A.is_equal)
     if rank < mate:
-        e_made = picks([e_zero], T.wf[:, 3:67:4])
+        e_made = picks([], T.wf[:, 3:67:4])
         e_wf, e_le, table = e_made, e_shared, T.wf
     else:
         e_made = event()
         for h in range(2):
-            V([e_zero], ts, T.le[:, 17 * h:17 * h + 15:2], T.yy[:, 0:32:4], T.pgf[:, 0:1], 8.0, A.subtract, A.is_equal, ev=e_made)
+            V([e_col2], ts, T.le[:, 17 * h:17 * h + 15:2], T.yy[:, 0:32:4], T.pgf[:, 0:1], None, A.is_equal, ev=e_made)
         e_wf, e_le, table = e_shared, e_made, T.le
     use("G", [e_made])
     g.remote_dma_fused([RemoteDMATransfer(dst_ids=[dst_id(mate)], dma_engine_mask=bits(eng), remote_sem=T.sem.shared,
                                           srcs=[table[:, :]], dsts=[table[:, :]])], local_sem=T.sem.ssent)
-    e_yrot = event()
-    for t, q, d, n in runs:
-        iota_f(T.yrot[:, 32 * t:32 * t + 32 * n], [[32 * d, n], [1, 32]], 32 * q, ev=e_yrot)
-    e_rfree = iota_f(T.rfree[0:16, :], [[0, 8], [1, 16]], 128)
+    e_yb = iota_f(T.yb[:, :], [[4, 4], [16, 2], [1, 4]], 0)
 
-    e_dgm = V([e_zero, e_xx], ts, T.dgm[:, :], T.xx[:, :], T.c4[:, 0:1], -16384.0, A.not_equal, A.mult)
-    e_l = V([e_vi], ts, T.lw[:, 12:140], T.vi[:, :], T.pgf[:, 0:1], None, A.is_equal)
-    e_tq = V([e_tp], vec.transpose, T.tq[:, :], T.tp[:, :])
+    place = T.posb[:, :].indirect(T.offp[:, 0:2])
+    e_dxy = V([e_posb, e_col2, e_xyw], tt, T.dxy[:, :], place, T.xyw[:, :], A.subtract)
+    e_off2 = V([e_cv], ts, T.off2[:, :], T.yy[:, 0:64:4], 0.125, T.cv[:, 0:1], A.mult, A.add)
+    e_sqw = V([e_dxy], tt, T.sqw[:, :], T.dxy[:, :], T.dxy[:, :], A.mult)
+    e_tq = event()
+    V([e_tp[0]], vec.transpose, T.tq[:, 0:128], T.tp[:, 0:128], ev=e_tq)
+    e_d2w = V([e_sqw], tt, T.d2w[:, :], T.sqw[:, 0:16], T.sqw[:, 16:32], A.add)
+    V([e_tp[1]], vec.transpose, T.tq[:, 128:256], T.tp[:, 128:256], ev=e_tq)
+    e_dg = act([], T.dg[:, :], T.xx[:, :], F.Square, bias=T.c4[:, 0:1], scale=-1.0)
+    e_seg = act([], T.seg[:, :], T.xx[:, :], F.Relu, bias=9 * 2.0 ** 20, scale=-2.0 ** 20)
+    e_r128 = act([], T.r128[:, 0:1], T.rf[:, 0:1], F.Copy, bias=128.0)
+    e_dgm = act([e_dg], T.dgm[:, :], T.dg[:, :], F.Copy, scale=64.0)
     e_taut = act([e_tq, e_off2], T.taut[:, :], T.tq[:, :].indirect(T.off2[:, :]), F.Copy)
 
-    d2i = lambda q: V([e_sy, e_sx[q]], tt, T.d2i[:, 64 * q:64 * q + 64], p[1][:, 0:64], T.sx[:, 64 * q:64 * q + 64], A.add)
-    half = lambda buf, k: buf[:, 128 * k:128 * k + 128]
-    hi = lambda k: V(e_d2i[2 * k:2 * k + 2], ts, half(T.hi, k), half(T.d2i, k), 5, 15, A.arith_shift_right, A.bitwise_and)
-    hm = lambda k: V([e_hi[k]], ts, half(T.hm, k), half(T.hi, k), T.rf[:, 0:1], None, A.is_equal)
-    e_d2i = [d2i(0), d2i(1)]
-    e_d2w = V([e_sqw], tt, T.d2w[:, :], T.sqx[:, :], T.sqy[:, :], A.add)
-    e_hi = [hi(0)]
-    e_lo32 = V([e_d2w], ts, T.lo32[:, :], T.d2w[:, :], 9, None, A.arith_shift_right)
-    e_d2i += [d2i(2), d2i(3)]
-    e_hm = [hm(0)]
+    e_hi32 = V([e_d2w], ts, T.hi32[:, :], T.d2w[:, :], 5, 15, A.arith_shift_right, A.bitwise_and)
+    e_lo32 = V([], ts, T.lo32[:, :], T.d2w[:, :], 9, None, A.arith_shift_right)
+    e_l = V([e_vi], ts, T.lw[:, 12:140], T.vi[:, :], T.pgf[:, 0:1], None, A.is_equal)
+    e_hi = V([e_hi32], cp, T.hi[:, :], T.hi32[:, :])
     e_lo = V([e_lo32], cp, T.lo[:, :], T.lo32[:, :])
-    e_hi.append(hi(1))
-    prod = lambda k: V([e_hm[k], e_lo, e_taut], tt, half(T.prod, k), T.taut[:, :].indirect(T.lo[:, 8 * k:8 * k + 8]), half(T.hm, k), A.mult)
-    e_prod = [prod(0)]
-    e_hm.append(hm(1))
-    e_prod.append(prod(1))
-    e_seg = V([], ts, T.seg[:, :], T.xx[:, :], 8.0, None, A.not_equal)
-    e_wd0 = V([], vec.memset, T.wd[:, :], 0.0)
+    mask = lambda q0, q1: (T.hm[:, 64 * q0:64 * q1], T.wd[:, 16:32].indirect(T.hi[:, 4 * q0:4 * q1]))
+    e_hm = [V([e_hi, e_wd], cp, *mask(0, 1)), act([e_hi, e_wd], *mask(1, 2), F.Copy), act([], *mask(2, 4), F.Copy)]
+    e_np = V([], ts, T.negp[:, :], place, -1.0, None, A.mult)
+    nx, ny = T.negp[:, 0:1], T.negp[:, 16:17]
+    e_prod = []
+    for k, (q0, q1) in enumerate(((0, 1), (1, 2), (2, 4))):
+        e = V([e_hm[k], e_lo, e_taut], tt, T.prod[:, 64 * q0:64 * q1], T.taut[:, :].indirect(T.lo[:, 4 * q0:4 * q1]), T.hm[:, 64 * q0:64 * q1], A.mult)
+        e_prod += [e] * (q1 - q0)
     e_tauo = V([], cp, T.tauo[:, :], T.taut[:, :])
-    e_wd = picks([e_wd0], T.wd[:, 16:32])
     use("P", [e_dgm, e_ident])
     pe.matmul(p[2][:, 0:64], T.ident[:, :], T.dgm[:, :], start=True, stop=False)
     for q in range(4):
-        use("P", [e_prod[q // 2], e_l])
+        use("P", [e_prod[q], e_l])
         mm = pe.matmul(p[2][:, 0:64], T.lw[:, 12 - 4 * q:140 - 4 * q], T.prod[:, 64 * q:64 * q + 64], start=False, stop=q == 3)
     e_s = run("P", [], lambda: mm)
+
+    e_byq = act([e_np], T.byq[:, :], T.yy[:, 0:64:8], F.Identity, bias=ny)
+    e_dxc = act([e_r128], T.dxc[:, 0:1], T.r128[:, 0:1], F.Identity, bias=nx)
+    e_dx2 = act([], T.dx2[:, 0:1], T.r128[:, 0:1], F.Square, bias=nx)
+    e_idf = act([e_ident], T.identf[:, :], T.ident[:, :], F.Copy)
+    e_dxs = act([e_dx2], T.dxs[:, 0:1], T.dx2[:, 0:1], F.Copy, bias=-15.5 / 32, scale=1.0 / 32)
+    e_dy2 = event()
+    for t, q in enumerate(order):
+        act([e_byq, e_yb], T.dy2[:, 32 * t:32 * t + 32], T.yb[:, :], F.Square, ev=e_dy2, bias=T.byq[:, q:q + 1])
     e_more = event()
-    V([], ts, T.xq[0:8, :], T.ones[0:8, 0:16], T.posf[0:8, 0:1], 0.125, A.mult, A.mult, ev=e_more)
+    V([e_dxc, e_ones], ts, T.xq[:, :], T.ones[:, 0:16], T.dxc[:, 0:1], 0.125, A.mult, A.mult, ev=e_more)
     V([], vec.memset, T.eights[0:16, :], 8.0, ev=e_more)
     V([], vec.memset, T.one16[0:16, :], 1.0, ev=e_more)
     V([], vec.memset, T.run[0:16, 16:24], 3.0e7, ev=e_more)
-    e_runq = V([e_s, e_seg], vec.tensor_tensor_scan, T.runq[:, :], T.seg[:, :], p[2][:, 0:64], 0.0, A.mult, A.max)
+    e_runq = V([e_s, e_seg], vec.tensor_tensor_scan, T.runq[:, :], T.seg[:, :], p[2][:, 0:64], 0.0, A.add, A.min)
     e_nl = V([e_runq], cp, T.nl[:, :], T.runq[:, 3:64:4])
-
-    e_dx2 = act([], T.dx2[:, 0:1], T.rf[:, 0:1], F.Square, bias=T.bx[:, 3:4])
-    e_idf = act([e_ident], T.identf[:, :], T.ident[:, :], F.Copy)
-    e_dxs = act([e_dx2], T.dxs[:, 0:1], T.dx2[:, 0:1], F.Copy, bias=-15.5 / 32, scale=1.0 / 32)
-    e_dy2 = act([e_yrot], T.dy2[:, :], T.yrot[:, :], F.Square, bias=ny)
+    e_pq = run("P", [e_more], lambda: pe.matmul(p[4][0:16, 0:128], T.xq[:, :], T.ident[:, :], start=True, stop=True))
     e_dy2s = act([e_dxs, e_dy2], T.dy2s[:, :], T.dy2[:, :], F.Identity, bias=T.dxs[:, 0:1], scale=1.0 / 32)
+    e_lxa = act([e_pq], T.lxa[0:16, :], p[4][0:16, 0:128], F.Copy)
     parts = [(0, 64), (64, 256)]
-    e_rf8 = act([e_rfree], T.rf8[0:16, :], T.rfree[0:16, :], F.Copy, scale=0.125)
-    e_pq = run("P", [e_more], lambda: pe.matmul(p[4][0:16, 0:128], T.xq[0:8, :], T.e8[0:8, :], start=True, stop=True))
 
+    e_n, at_n = {q: event() for q in "VS"}, [0]
+
+    def nat(q, n):
+        j = at_n[0]
+        at_n[0] += n
+        o, i = T.nat[:, j:j + n], T.trs[:, :].indirect(T.tauo[:, j // 16:(j + n) // 16])
+        if n and q == "V":
+            V([e_tr, e_tauo], cp, o, i, ev=e_n[q])
+        elif n:
+            act([e_tr, e_tauo], o, i, F.Copy, ev=e_n[q])
+
+    nat("S", NAT_S[0])
     e_va = [act([e_tr, e_nl], T.vc[:, 64 * k:64 * k + 64], T.trs[:, :].indirect(T.nl[:, 4 * k:4 * k + 4]), F.Copy) for k in (0, 1)]
     e_vv = [V([e_tr, e_nl], cp, T.vc[:, 64 * k:64 * k + 64], T.trs[:, :].indirect(T.nl[:, 4 * k:4 * k + 4])) for k in (2, 3)]
-    e_lxa = V([e_pq, e_rf8], tt, T.lxa[0:16, :], T.rf8[0:16, :], p[4][0:16, 0:128], A.subtract)
-    use("P", [e_wd])
+    nat("V", NAT_V[0])
     for k in (0, 1, 4, 5, 2, 3, 6, 7):
         use("P", [(e_va + e_vv)[k // 2]])
         o = 32 * (k // 2)
@@ -236,24 +235,11 @@ def rank_program(g, core, T, topo):
     g.remote_dma_fused([RemoteDMATransfer(dst_ids=[dst_id(q) for q in others], dma_engine_mask=bits(eng), remote_sem=T.sem["carr%d" % rank],
                                           srcs=[T.cland[:, own]], dsts=[T.cland[:, own] for q in others])], local_sem=T.sem.csent)
     e_em = event()
-    for t, q, d, n in runs:
-        sel([e_more], T.em[0:16, 32 * t:32 * t + 32 * n], T.eights[0:16, 0:32 * n], [[-2 * d, n], [-1, 2], [0, 16]], A.is_equal, -2 * q, 1, ev=e_em)
+    for t, q in enumerate(order):
+        sel([e_more], T.em[0:16, 32 * t:32 * t + 32], T.eights[0:16, :], [[0, 4], [-1, 2], [0, 4]], A.is_equal, -2 * q, 1, ev=e_em)
     e_wc = iota_f(T.wc[0:1, :], [[16, 16]], 8)
-
-    e_n, at_n = {q: event() for q in "VS"}, [0]
-
-    def nat(q, n):
-        j = at_n[0]
-        at_n[0] += n
-        o, i = T.nat[:, j:j + n], T.trs[:, :].indirect(T.tauo[:, j // 16:(j + n) // 16])
-        if q == "V":
-            V([e_tr, e_tauo], cp, o, i, ev=e_n[q])
-        else:
-            act([e_tr, e_tauo], o, i, F.Copy, ev=e_n[q])
-
-    for n in NAT_V:
-        nat("V", n)
-    nat("S", NAT_S[0])
+    nat("V", NAT_V[1])
+    nat("S", NAT_S[1])
 
     use("P", [e_own])
     pe.matmul(p[5][:, 0:32], T.ident[:, :], T.cland[:, own], start=True, stop=False)
@@ -265,108 +251,98 @@ def rank_program(g, core, T, topo):
         mm = pe.matmul(p[5][:, 0:32], T.ident[:, :], T.cland[:, 32 * q:32 * q + 32], start=False, stop=q == senders[N - 2])
     e_tot = run("P", [], lambda: mm)
     e_sq = act([e_tot], T.sq[:, :], p[5][:, 0:32], F.Square)
-    nat("S", NAT_S[1])
+    nat("S", NAT_S[2])
     e_e = chain([e_sq, e_le, e_lxa], [lambda: pe.matmul(p[4][0:16, 0:16], T.le[:, 0:16], T.sq[:, 0:16], start=True, stop=False),
                                       lambda: pe.matmul(p[4][0:16, 0:16], T.le[:, 16:32], T.sq[:, 16:32], start=False, stop=True)])
     e_run = V([e_e, e_more], vec.tensor_tensor_scan, T.run[0:16, 0:16], T.one16[0:16, :], p[4][0:16, 0:16], 0.0, A.mult, A.max)
+    nat("V", NAT_V[2])
     ac = T.acol[0:16, 0:1]
     e_ac = act([e_run], T.lt[0:16, :], T.run[0:16, :], F.Sign, bias=T.run[0:16, 15:16], scale=-1.0, accum_out=ac)
-    nat("S", NAT_S[2])
+    nat("S", NAT_S[3])
     e_lh = V([e_ac, e_lxa], ts, T.lh[0:16, :], T.lxa[0:16, :], ac, ac, A.add, A.mult)
+    nat("V", NAT_V[3])
     e_d = [chain([e_lh, e_em], [lambda: pe.matmul(p[6 + k][:, 0:c1 - c0], T.lh[0:16, :], T.em[0:16, c0:c1], start=False, stop=True)])
            for k, (c0, c1) in enumerate(parts)]
 
-    e_sel = {}
+    lists = lambda k: V([e_d[k]], cp, T.flist[:, parts[k][0]:parts[k][1]], p[6 + k][:, 0:parts[k][1] - parts[k][0]])
+    e_sel = [lists(0)]
+    banks = [p[k] for k in range(len(GROUPS) - 1)] + [p[4]]
+    at = {t: (k, tts.index(t)) for k, tts in enumerate(GROUPS) for t in tts}
+    gathered, summed, e_pt, last = [], [], {}, [None]
+    for bank in (p[4], p[5]):
+        pe.matmul(bank[:, 0:64], T.wd[:, 32:160], T.ident[:, 0:64], start=True, stop=False)
 
-    def select(k):
-        t0, t1 = parts[k][0] // 32, parts[k][1] // 32
-        e = V([e_d[k]], cp, T.flist[:, 32 * t0:32 * t1], p[6 + k][:, 0:32 * (t1 - t0)])
-        for t in range(t0, t1):
-            e_sel[t] = e
-
-    groups = [[0], [1], [2, 3], [4, 5], [6]]
-    banks = [p[0], p[1], p[2], p[3], p[4]]
-    at = {t: (k, tts.index(t)) for k, tts in enumerate(groups) for t in tts}
-    e_f = {t: [] for t in range(N)}
-
-    def gather(q, t, j0=0, j1=512):
-        o = T.ff[:, 512 * t + j0:512 * t + j1]
-        i = T.nat[:, :].indirect(T.flist[:, 32 * t + j0 // 16:32 * t + j1 // 16])
-        w = [e_n["V"], e_n["S"], e_sel[t]]
-        e_f[t].append((j0, V(w, lambda: cp(o, i)) if q == "V" else act(w, o, i, F.Copy)))
-
-    e_pt, last = {}, [None]
+    def gather(q, j0, j1):
+        o = T.ff[:, j0:j1]
+        i = T.nat[:, :].indirect(T.flist[:, j0 // 16:j1 // 16])
+        w = [e_n["V"], e_n["S"]] + [e_sel[k] for k, (c0, c1) in enumerate(parts) if j0 < 16 * c1 and j1 > 16 * c0]
+        gathered.append((j0, j1, V(w, lambda: cp(o, i)) if q == "V" else act(w, o, i, F.Copy)))
 
     def collect(k):
-        pe.wait_ge(T.sem["far%d" % k], len(eng) // len(groups[k]) * len(groups[k]))
-        for t in groups[k]:
-            last[0] = pe.matmul(p[5][0:64, 0:128], T.fland[:, 64 * senders[t]:64 * senders[t] + 64], T.ident[:, :], start=t == 0, stop=t == N - 2)
+        pe.wait_ge(T.sem["far%d" % k], len(eng))
+        for t in GROUPS[k]:
+            for h in range(2):
+                last[0] = pe.matmul(p[5][64 * h:64 * h + 64, 0:64], T.fland[:, 64 * senders[t]:64 * senders[t] + 64], T.ident[:, 64 * h:64 * h + 64],
+                                    start=False, stop=t == N - 3)
 
-    def sensors(t):
-        for c in range(4):
-            use("P", [e for j0, e in e_f[t] if j0 < 128 * c + 128] + [e_wd])
-            f = T.ff[:, 512 * t + 128 * c:512 * t + 128 * c + 128]
-            if t == N - 1:
+    def sensors(u):
+        t, c = u // 4, u % 4
+        summed.append(u)
+        done = all(4 * t + x in summed for x in range(4))
+        for h in range(2 if t >= N - 2 else 1):
+            j0, j1 = (128 * u + 64 * h, 128 * u + 64 * h + 64) if t >= N - 2 else (128 * u, 128 * u + 128)
+            use("P", [e for i0, i1, e in gathered if i0 < j1 and i1 > j0])
+            if t >= N - 2:
                 use("P", [e_wf])
-                pe.matmul(p[5][0:64, 0:128], T.wf[:, 3 - c:67 - c], f, start=False, stop=False)
+                mm = pe.matmul(p[t - 2][64 * h:64 * h + 64, 0:64], T.wf[:, 3 - c:67 - c], T.ff[:, j0:j1], start=False, stop=t == N - 2 and done)
             else:
                 o = 64 * at[t][1]
-                mm = pe.matmul(banks[at[t][0]][:, o + c:o + 64:4], f, T.wd[:, 16:32], start=True, stop=True)
-        if t < N - 1:
+                mm = pe.matmul(banks[at[t][0]][:, o + c:o + 64:4], T.ff[:, j0:j1], T.wd[:, 16:32], start=True, stop=True)
+        if done and t < N - 1:
             e_pt[t] = run("P", [], lambda: mm)
 
-    def send(k):
-        tts = groups[k]
-        e = V([e_pt[t] for t in tts], cp, T.fsend[:, 64 * tts[0]:64 * tts[-1] + 64], banks[k][:, 0:64 * len(tts)])
+    def send(q, k):
+        tts = GROUPS[k]
+        w, o, i = [e_pt[t] for t in tts], T.fsend[:, 64 * tts[0]:64 * tts[-1] + 64], banks[k][:, 0:64 * len(tts)]
+        e = V(w, cp, o, i) if q == "V" else act(w, o, i, F.Copy)
         use("G", [e])
         n = len(eng) // len(tts)
         g.remote_dma_fused([RemoteDMATransfer(dst_ids=[dst_id(order[t])], dma_engine_mask=bits(eng[n * i:n * i + n]), remote_sem=T.sem["far%d" % k],
                                               srcs=[T.fsend[:, 64 * t:64 * t + 64]], dsts=[T.fland[:, 64 * rank:64 * rank + 64]])
                             for i, t in enumerate(tts)], local_sem=T.sem.fsent)
 
-    select(0)
-    gather("V", 0, 0, 256)
-    gather("S", 0, 256, 512)
-    sensors(0)
-    select(1)
-    gather("V", 1, 0, 256)
-    gather("S", 1, 256, 512)
-    send(0)
-    sensors(1)
-    gather("S", 2)
-    sensors(2)
-    gather("V", 3)
-    send(1)
-    sensors(3)
-    gather("S", 4)
-    sensors(4)
-    gather("V", 5, 0, 320)
-    send(2)
-    gather("S", 5, 320, 512)
-    sensors(5)
-    gather("V", 6, 0, 256)
-    gather("S", 6, 256, 512)
-    send(3)
-    sensors(6)
-    send(4)
-    gather("V", 7, 0, 128)
-    gather("S", 7, 128, 512)
+    for step in PLAN:
+        if step == "lists":
+            e_sel.append(lists(1))
+        elif len(step) == 2:
+            send(*step)
+        else:
+            gather(*step)
+            for u in range(4 * (N - 1)):
+                if u not in summed and sum(max(0, min(j1, 128 * u + 128) - max(j0, 128 * u)) for j0, j1, e in gathered) == 128:
+                    sensors(u)
     e_w1 = chain([e_ac, e_idf, e_sel[0]], [lambda: pe.matmul(p[6][0:1, 0:16], ac, T.identf[0:16, 0:16], start=True, stop=True)])
-    collect(0)
-    collect(1)
-    sensors(7)
+    early = 1
+    for k in range(early):
+        collect(k)
+    for u in range(4 * (N - 1), 4 * N):
+        sensors(u)
     e_w2 = V([e_w1, e_wc], tt, T.w2[0:1, :], p[6][0:1, 0:16], T.wc[0:1, :], A.add)
     e_w = run("Y", [e_w2], lambda: g.sync.dma_start(T.w[:, :], T.w2[0:1, :]), inc=16)
 
-    for k in range(2, len(groups)):
+    for k in range(early, len(GROUPS) - 1):
         collect(k)
     e_fin = run("P", [], lambda: last[0])
-    e_y = V([e_fin], cp, T.ysb[0:64, :], p[5][0:64, 0:128])
-    e_st = run("Y", [e_y], lambda: g.sync.dma_start(T.y[:, :], T.ysb[0:64, :]), inc=16)
+    use("V", [e_fin])
+    vec.wait_ge(T.sem["far%d" % (len(GROUPS) - 1)], len(eng))
+    e_y = V([], tt, T.ysb[:, :], p[5][:, 0:64], T.fland[:, 64 * mate:64 * mate + 64], A.add)
+    e_st = event()
+    for h in range(2):
+        run("YS"[h], [e_y], lambda: (g.sync, sca)[h].dma_start(T.y[:, 256 * h:256 * h + 256], T.ysb[64 * h:64 * h + 64, :]), ev=e_st, inc=16)
     use("Y", [e_w, e_st])
     g.wait_ge(T.sem.ssent, len(eng))
     g.wait_ge(T.sem.csent, len(eng))
-    g.wait_ge(T.sem.fsent, len(groups) * len(eng))
+    g.wait_ge(T.sem.fsent, len(GROUPS) * len(eng))
     for e in events:
         if not e["used"]:
             g.wait_ge(e["sem"], e["total"])

from concourse.bass import DstId, RemoteDMATransfer
from concourse.mybir import AluOpType as A, ActivationFunctionType as F

_SB = {
    "int32": "posi 16 posb 16 tz 256 vi 128 pgi 2 pg2 2 pcol 2 rcol 2 r4 2 r12 2 i16 16 d2w 16 lo32 16 hi32 16",
    "uint16": "tauo 256 lo 16 hi 16 nl 16 flist 256 off1 16 off2 16 offp 2",
    "bfloat16": "trs 8192 nat 4096 ones 128 eights 32 ident 128 wd 160 wf 80 vc 256 cland 256 xq 16 lxa 128 em 256 dgm 64 hm 256 "
                "ff 4096 fsend 448 fland 512",
    "float16": "lh 128",
    "float32": "negp 32 lw 140 pgf 2 rf 2 r8 2 r128 2 c4 2 c12 2 cv 2 yy 64 xx 64 xyw 32 dxy 32 sqw 32 yb 32 byq 8 "
               "prod 256 dg 64 seg 64 runq 64 dy2 256 dy2s 256 dxc 2 dx2 2 dxs 2 le 32 identf 128 sq 32 "
               "one16 16 tp 256 tq 256 taut 256 run 24 lt 24 acol 2 wc 16 w2 16 ysb 64",
}
SCRATCH = {"p%d" % _k: ("psum", [128, 512], "float32") for _k in range(8)}
for _d in _SB:
    _l = _SB[_d].split()
    for _k in range(0, len(_l), 2):
        SCRATCH[_l[_k]] = ("sbuf", [128, int(_l[_k + 1])], _d)
SEMAPHORES = ["carr%d" % _k for _k in range(8)] + ["far%d" % _k for _k in range(7)] + ["csent", "fsent", "shared", "ssent"] + ["e%d" % _k for _k in range(130)]

NAT_V, NAT_S = [128, 1600, 96, 160], [0, 1664, 160, 288]
GROUPS = [[0], [1, 2], [3, 4], [5], [6]]
PLAN = ["lists", ("V", 0, 256), ("S", 256, 544), ("V", 544, 896), ("V", 0), ("S", 896, 1536), ("V", 1536, 2048), ("V", 1),
        ("S", 2048, 2560), ("V", 2560, 2816), ("S", 2816, 3072), ("V", 3072, 3264), ("V", 2), ("S", 3264, 3392), ("V", 3392, 3488), ("V", 3),
        ("S", 3488, 3584), ("V", 3584, 3744), ("V", 4), ("S", 3744, 4096)]


def rank_program(g, core, T, topo):
    rank = T.rank_of(core)
    if rank is None:
        return
    N = len(T.cores)
    vec, sca, pe = g.vector, g.scalar, g.tensor
    queues = {"G": g, "V": vec, "S": sca, "P": pe, "Y": g.sync}
    known = {q: set() for q in queues}
    events = []

    def event():
        e = {"n": len(events), "sem": T.sem["e%d" % len(events)], "total": 0, "knows": set(), "used": False}
        events.append(e)
        return e

    def use(q, waits):
        for e in waits:
            if e["n"] not in known[q]:
                queues[q].wait_ge(e["sem"], e["total"])
                e["used"] = True
                known[q] |= e["knows"] | {e["n"]}

    def run(q, waits, call, ev=None, inc=1):
        use(q, waits)
        e = event() if ev is None else ev
        assert not e["used"]
        call().then_inc(e["sem"], inc)
        e["total"] += inc
        e["knows"] |= known[q]
        return e

    def V(waits, fn, *a, **k):
        return run("V", waits, lambda: fn(*a), **k)

    ts, tt, cp = vec.tensor_scalar, vec.tensor_tensor, vec.tensor_copy
    act = lambda waits, out, in_, func, ev=None, **k: run("S", waits, lambda: sca.activation(out, in_, func, **k), ev=ev)

    def chain(waits, mms):
        use("P", waits)
        for m in mms:
            last = m()
        return run("P", [], lambda: last)

    p = [T["p%d" % k] for k in range(8)]

    e_pos = run("Y", [], lambda: g.sync.dma_start(T.posi[0:1, :], T.pos[:, :]), inc=16)
    e_tau = event()
    for o in range(2):
        run("SY"[o], [], lambda: (sca, g.sync)[o].dma_start(T.tz[:, 128 * o:128 * o + 128], T.tau[o:8:2, :]), ev=e_tau, inc=16)
    e_tr = run("Y", [], lambda: g.sync.dma_start(T.trs[:, :], T.tr[:, :]), inc=16)

    def kind(a, b):
        a, b = topo.chip(T.cores[a]), topo.chip(T.cores[b])
        return 2 if topo.mates(a, b) else 1 if topo.same_plane(a, b) else 0

    def ordered(r):
        return sorted([q for q in range(N) if q != r], key=lambda q: (kind(r, q), (q - r) % N)) + [r]

    order = ordered(rank)
    others, mate = order[:-1], order[-2]
    senders = [[q for q in range(N) if ordered(q)[t] == rank][0] for t in range(N)]

    def dst_id(q):
        rid, pid, _ = topo.addr(T.cores[q])
        return DstId(rid=rid, pnc=pid)

    def bits(es):
        m = 0
        for e in es:
            m |= 1 << e
        return m

    eng = [e for e in topo.engines(core, T.cores[mate]) if all(e in topo.engines(core, T.cores[q]) for q in others)]

    iota_i = lambda out, pat, base, cm: run("G", [], lambda: g.iota(out, pat, base, cm))
    iota_f = lambda out, pat, base, ev=None: run("G", [], lambda: g.iota(out, pat, base, 0, allow_small_or_imprecise_dtypes=True), ev=ev)
    sel = lambda waits, out, in_, pat, op, base, cm, ev=None: run("G", waits, lambda: g.affine_select(out, in_, pat, op, 0.0, base, cm), ev=ev)
    e_fill = event()
    V([], vec.memset, T.wd[:, :], 0.0, ev=e_fill)
    V([], vec.memset, T.lw[:, 0:12], 0.0, ev=e_fill)
    e_pcol = iota_i(T.pcol[:, 0:1], [[1, 1]], 0, 1)
    e_i16 = iota_i(T.i16[:, :], [[16, 8], [128, 2]], 0, 0)
    e_yy = iota_f(T.yy[:, :], [[16, 16], [0, 4]], 0)
    e_xx = iota_f(T.xx[:, :], [[0, 16], [16, 4]], 8)
    e_posb = run("G", [e_pos], lambda: g.partition_broadcast(T.posb[:, :], T.posi[0:1, :], 128))
    e_vi = iota_i(T.vi[:, :], [[16, 8], [128, 4], [0, 4]], 0, 0)

    e_bits = event()
    V([e_pcol], ts, T.rcol[:, 0:1], T.pcol[:, 0:1], 15, None, A.bitwise_and, ev=e_bits)
    V([], ts, T.r4[:, 0:1], T.pcol[:, 0:1], 3, None, A.bitwise_and, ev=e_bits)
    V([], ts, T.r12[:, 0:1], T.pcol[:, 0:1], 12, None, A.bitwise_and, ev=e_bits)
    V([], ts, T.pg2[:, 0:1], T.pcol[:, 0:1], 3, 14, A.arith_shift_right, A.bitwise_and, ev=e_bits)
    e_ones = V([], vec.memset, T.ones[:, :], 1.0)
    V([], vec.memset, T.wf[:, :] if rank < mate else T.le[:, :], 0.0, ev=e_fill)
    e_cols = event()
    V([e_bits], cp, T.rf[:, 0:1], T.rcol[:, 0:1], ev=e_cols)
    V([], ts, T.c4[:, 0:1], T.r4[:, 0:1], 16.0, 8.0, A.mult, A.add, ev=e_cols)
    V([], ts, T.c12[:, 0:1], T.r12[:, 0:1], 4.0, -24.0, A.mult, A.add, ev=e_cols)
    V([], ts, T.r8[:, 0:1], T.rcol[:, 0:1], 8.0, -255.0, A.is_ge, A.mult, ev=e_cols)
    e_col2 = event()
    for o in range(2):
        V([], ts, T.offp[:, o:o + 1], T.pg2[:, 0:1], float(o), None, A.add, ev=e_col2)
    V([], ts, T.pgf[:, 0:1], T.pg2[:, 0:1], 8.0, None, A.mult, ev=e_col2)
    e_off1 = V([e_cols, e_i16], ts, T.off1[:, :], T.i16[:, :], T.rf[:, 0:1], None, A.add)
    e_ident = sel([e_ones], T.ident[:, :], T.ones[:, :], [[-1, 128]], A.is_equal, 0, 1)
    picks = lambda waits, out: V(waits, ts, out, T.yy[:, 0:64:4], 1.0 / 16, T.rf[:, 0:1], A.mult, A.is_equal)
    e_wd = picks([e_fill, e_yy], T.wd[:, 16:32])
    e_xyw = event()
    act([e_cols, e_yy], T.xyw[:, 0:16], T.yy[:, 0:16], F.Identity, ev=e_xyw, bias=T.c4[:, 0:1], scale=4.0)
    act([e_xx], T.xyw[:, 16:32], T.xx[:, 0:16], F.Identity, ev=e_xyw, bias=T.c12[:, 0:1], scale=4.0)
    e_cv = act([], T.cv[:, 0:1], T.rf[:, 0:1], F.Identity, bias=T.r8[:, 0:1], scale=32.0)

    e_tp = [act([e_tau, e_off1], T.tp[:, 128 * k:128 * k + 128], T.tz[:, :].indirect(T.off1[:, 8 * k:8 * k + 8]), F.Copy) for k in range(2)]

    e_shared = {"n": len(events), "sem": T.sem.shared, "total": len(eng), "knows": set(), "used": False}
    events.append(e_shared)
    if rank < mate:
        e_made = picks([], T.wf[:, 3:67:4])
        e_wf, e_le, table = e_made, e_shared, T.wf
    else:
        e_made = event()
        for h in range(2):
            V([e_col2], ts, T.le[:, 17 * h:17 * h + 15:2], T.yy[:, 0:32:4], T.pgf[:, 0:1], None, A.is_equal, ev=e_made)
        e_wf, e_le, table = e_shared, e_made, T.le
    use("G", [e_made])
    g.remote_dma_fused([RemoteDMATransfer(dst_ids=[dst_id(mate)], dma_engine_mask=bits(eng), remote_sem=T.sem.shared,
                                          srcs=[table[:, :]], dsts=[table[:, :]])], local_sem=T.sem.ssent)
    e_yb = iota_f(T.yb[:, :], [[4, 4], [16, 2], [1, 4]], 0)

    place = T.posb[:, :].indirect(T.offp[:, 0:2])
    e_dxy = V([e_posb, e_col2, e_xyw], tt, T.dxy[:, :], place, T.xyw[:, :], A.subtract)
    e_off2 = V([e_cv], ts, T.off2[:, :], T.yy[:, 0:64:4], 0.125, T.cv[:, 0:1], A.mult, A.add)
    e_sqw = V([e_dxy], tt, T.sqw[:, :], T.dxy[:, :], T.dxy[:, :], A.mult)
    e_tq = event()
    V([e_tp[0]], vec.transpose, T.tq[:, 0:128], T.tp[:, 0:128], ev=e_tq)
    e_d2w = V([e_sqw], tt, T.d2w[:, :], T.sqw[:, 0:16], T.sqw[:, 16:32], A.add)
    V([e_tp[1]], vec.transpose, T.tq[:, 128:256], T.tp[:, 128:256], ev=e_tq)
    e_dg = act([], T.dg[:, :], T.xx[:, :], F.Square, bias=T.c4[:, 0:1], scale=-1.0)
    e_seg = act([], T.seg[:, :], T.xx[:, :], F.Relu, bias=9 * 2.0 ** 20, scale=-2.0 ** 20)
    e_r128 = act([], T.r128[:, 0:1], T.rf[:, 0:1], F.Copy, bias=128.0)
    e_dgm = act([e_dg], T.dgm[:, :], T.dg[:, :], F.Copy, scale=64.0)
    e_taut = act([e_tq, e_off2], T.taut[:, :], T.tq[:, :].indirect(T.off2[:, :]), F.Copy)

    e_hi32 = V([e_d2w], ts, T.hi32[:, :], T.d2w[:, :], 5, 15, A.arith_shift_right, A.bitwise_and)
    e_lo32 = V([], ts, T.lo32[:, :], T.d2w[:, :], 9, None, A.arith_shift_right)
    e_l = V([e_vi], ts, T.lw[:, 12:140], T.vi[:, :], T.pgf[:, 0:1], None, A.is_equal)
    e_hi = V([e_hi32], cp, T.hi[:, :], T.hi32[:, :])
    e_lo = V([e_lo32], cp, T.lo[:, :], T.lo32[:, :])
    mask = lambda q0, q1: (T.hm[:, 64 * q0:64 * q1], T.wd[:, 16:32].indirect(T.hi[:, 4 * q0:4 * q1]))
    e_hm = [V([e_hi, e_wd], cp, *mask(0, 1)), act([e_hi, e_wd], *mask(1, 2), F.Copy), act([], *mask(2, 4), F.Copy)]
    e_np = V([], ts, T.negp[:, :], place, -1.0, None, A.mult)
    nx, ny = T.negp[:, 0:1], T.negp[:, 16:17]
    e_prod = []
    for k, (q0, q1) in enumerate(((0, 1), (1, 2), (2, 4))):
        e = V([e_hm[k], e_lo, e_taut], tt, T.prod[:, 64 * q0:64 * q1], T.taut[:, :].indirect(T.lo[:, 4 * q0:4 * q1]), T.hm[:, 64 * q0:64 * q1], A.mult)
        e_prod += [e] * (q1 - q0)
    e_tauo = V([], cp, T.tauo[:, :], T.taut[:, :])
    use("P", [e_dgm, e_ident])
    pe.matmul(p[2][:, 0:64], T.ident[:, :], T.dgm[:, :], start=True, stop=False)
    for q in range(4):
        use("P", [e_prod[q], e_l])
        mm = pe.matmul(p[2][:, 0:64], T.lw[:, 12 - 4 * q:140 - 4 * q], T.prod[:, 64 * q:64 * q + 64], start=False, stop=q == 3)
    e_s = run("P", [], lambda: mm)

    e_byq = act([e_np], T.byq[:, :], T.yy[:, 0:64:8], F.Identity, bias=ny)
    e_dxc = act([e_r128], T.dxc[:, 0:1], T.r128[:, 0:1], F.Identity, bias=nx)
    e_dx2 = act([], T.dx2[:, 0:1], T.r128[:, 0:1], F.Square, bias=nx)
    e_idf = act([e_ident], T.identf[:, :], T.ident[:, :], F.Copy)
    e_dxs = act([e_dx2], T.dxs[:, 0:1], T.dx2[:, 0:1], F.Copy, bias=-15.5 / 32, scale=1.0 / 32)
    e_dy2 = event()
    for t, q in enumerate(order):
        act([e_byq, e_yb], T.dy2[:, 32 * t:32 * t + 32], T.yb[:, :], F.Square, ev=e_dy2, bias=T.byq[:, q:q + 1])
    e_more = event()
    V([e_dxc, e_ones], ts, T.xq[:, :], T.ones[:, 0:16], T.dxc[:, 0:1], 0.125, A.mult, A.mult, ev=e_more)
    V([], vec.memset, T.eights[0:16, :], 8.0, ev=e_more)
    V([], vec.memset, T.one16[0:16, :], 1.0, ev=e_more)
    V([], vec.memset, T.run[0:16, 16:24], 3.0e7, ev=e_more)
    e_runq = V([e_s, e_seg], vec.tensor_tensor_scan, T.runq[:, :], T.seg[:, :], p[2][:, 0:64], 0.0, A.add, A.min)
    e_nl = V([e_runq], cp, T.nl[:, :], T.runq[:, 3:64:4])
    e_pq = run("P", [e_more], lambda: pe.matmul(p[4][0:16, 0:128], T.xq[:, :], T.ident[:, :], start=True, stop=True))
    e_dy2s = act([e_dxs, e_dy2], T.dy2s[:, :], T.dy2[:, :], F.Identity, bias=T.dxs[:, 0:1], scale=1.0 / 32)
    e_lxa = act([e_pq], T.lxa[0:16, :], p[4][0:16, 0:128], F.Copy)
    parts = [(0, 64), (64, 256)]

    e_n, at_n = {q: event() for q in "VS"}, [0]

    def nat(q, n):
        j = at_n[0]
        at_n[0] += n
        o, i = T.nat[:, j:j + n], T.trs[:, :].indirect(T.tauo[:, j // 16:(j + n) // 16])
        if n and q == "V":
            V([e_tr, e_tauo], cp, o, i, ev=e_n[q])
        elif n:
            act([e_tr, e_tauo], o, i, F.Copy, ev=e_n[q])

    nat("S", NAT_S[0])
    e_va = [act([e_tr, e_nl], T.vc[:, 64 * k:64 * k + 64], T.trs[:, :].indirect(T.nl[:, 4 * k:4 * k + 4]), F.Copy) for k in (0, 1)]
    e_vv = [V([e_tr, e_nl], cp, T.vc[:, 64 * k:64 * k + 64], T.trs[:, :].indirect(T.nl[:, 4 * k:4 * k + 4])) for k in (2, 3)]
    nat("V", NAT_V[0])
    for k in (0, 1, 4, 5, 2, 3, 6, 7):
        use("P", [(e_va + e_vv)[k // 2]])
        o = 32 * (k // 2)
        mm = pe.matmul(p[3][o:o + 32, 0:32], T.wd[:, 16 - 16 * (k % 2):48 - 16 * (k % 2)], T.vc[:, 32 * k:32 * k + 32], start=k % 2 == 0, stop=k % 2 == 1)
    e_cs = run("P", [], lambda: mm)
    own = slice(32 * rank, 32 * rank + 32)
    e_own = V([e_cs], cp, T.cland[:, own], p[3][:, 0:32])
    use("G", [e_own])
    g.remote_dma_fused([RemoteDMATransfer(dst_ids=[dst_id(q) for q in others], dma_engine_mask=bits(eng), remote_sem=T.sem["carr%d" % rank],
                                          srcs=[T.cland[:, own]], dsts=[T.cland[:, own] for q in others])], local_sem=T.sem.csent)
    e_em = event()
    for t, q in enumerate(order):
        sel([e_more], T.em[0:16, 32 * t:32 * t + 32], T.eights[0:16, :], [[0, 4], [-1, 2], [0, 4]], A.is_equal, -2 * q, 1, ev=e_em)
    e_wc = iota_f(T.wc[0:1, :], [[16, 16]], 8)
    nat("V", NAT_V[1])
    nat("S", NAT_S[1])

    use("P", [e_own])
    pe.matmul(p[5][:, 0:32], T.ident[:, :], T.cland[:, own], start=True, stop=False)
    use("P", [e_idf, e_dy2s])
    for k, (c0, c1) in enumerate(parts):
        pe.matmul(p[6 + k][:, 0:c1 - c0], T.identf[:, :], T.dy2s[:, c0:c1], start=True, stop=False)
    for q in senders[:-1]:
        pe.wait_ge(T.sem["carr%d" % q], len(eng))
        mm = pe.matmul(p[5][:, 0:32], T.ident[:, :], T.cland[:, 32 * q:32 * q + 32], start=False, stop=q == senders[N - 2])
    e_tot = run("P", [], lambda: mm)
    e_sq = act([e_tot], T.sq[:, :], p[5][:, 0:32], F.Square)
    nat("S", NAT_S[2])
    e_e = chain([e_sq, e_le, e_lxa], [lambda: pe.matmul(p[4][0:16, 0:16], T.le[:, 0:16], T.sq[:, 0:16], start=True, stop=False),
                                      lambda: pe.matmul(p[4][0:16, 0:16], T.le[:, 16:32], T.sq[:, 16:32], start=False, stop=True)])
    e_run = V([e_e, e_more], vec.tensor_tensor_scan, T.run[0:16, 0:16], T.one16[0:16, :], p[4][0:16, 0:16], 0.0, A.mult, A.max)
    nat("V", NAT_V[2])
    ac = T.acol[0:16, 0:1]
    e_ac = act([e_run], T.lt[0:16, :], T.run[0:16, :], F.Sign, bias=T.run[0:16, 15:16], scale=-1.0, accum_out=ac)
    nat("S", NAT_S[3])
    e_lh = V([e_ac, e_lxa], ts, T.lh[0:16, :], T.lxa[0:16, :], ac, ac, A.add, A.mult)
    nat("V", NAT_V[3])
    e_d = [chain([e_lh, e_em], [lambda: pe.matmul(p[6 + k][:, 0:c1 - c0], T.lh[0:16, :], T.em[0:16, c0:c1], start=False, stop=True)])
           for k, (c0, c1) in enumerate(parts)]

    lists = lambda k: V([e_d[k]], cp, T.flist[:, parts[k][0]:parts[k][1]], p[6 + k][:, 0:parts[k][1] - parts[k][0]])
    e_sel = [lists(0)]
    banks = [p[k] for k in range(len(GROUPS) - 1)] + [p[4]]
    at = {t: (k, tts.index(t)) for k, tts in enumerate(GROUPS) for t in tts}
    gathered, summed, e_pt, last = [], [], {}, [None]
    for bank in (p[4], p[5]):
        pe.matmul(bank[:, 0:64], T.wd[:, 32:160], T.ident[:, 0:64], start=True, stop=False)

    def gather(q, j0, j1):
        o = T.ff[:, j0:j1]
        i = T.nat[:, :].indirect(T.flist[:, j0 // 16:j1 // 16])
        w = [e_n["V"], e_n["S"]] + [e_sel[k] for k, (c0, c1) in enumerate(parts) if j0 < 16 * c1 and j1 > 16 * c0]
        gathered.append((j0, j1, V(w, lambda: cp(o, i)) if q == "V" else act(w, o, i, F.Copy)))

    def collect(k):
        pe.wait_ge(T.sem["far%d" % k], len(eng))
        for t in GROUPS[k]:
            for h in range(2):
                last[0] = pe.matmul(p[5][64 * h:64 * h + 64, 0:64], T.fland[:, 64 * senders[t]:64 * senders[t] + 64], T.ident[:, 64 * h:64 * h + 64],
                                    start=False, stop=t == N - 3)

    def sensors(u):
        t, c = u // 4, u % 4
        summed.append(u)
        done = all(4 * t + x in summed for x in range(4))
        for h in range(2 if t >= N - 2 else 1):
            j0, j1 = (128 * u + 64 * h, 128 * u + 64 * h + 64) if t >= N - 2 else (128 * u, 128 * u + 128)
            use("P", [e for i0, i1, e in gathered if i0 < j1 and i1 > j0])
            if t >= N - 2:
                use("P", [e_wf])
                mm = pe.matmul(p[t - 2][64 * h:64 * h + 64, 0:64], T.wf[:, 3 - c:67 - c], T.ff[:, j0:j1], start=False, stop=t == N - 2 and done)
            else:
                o = 64 * at[t][1]
                mm = pe.matmul(banks[at[t][0]][:, o + c:o + 64:4], T.ff[:, j0:j1], T.wd[:, 16:32], start=True, stop=True)
        if done and t < N - 1:
            e_pt[t] = run("P", [], lambda: mm)

    def send(q, k):
        tts = GROUPS[k]
        w, o, i = [e_pt[t] for t in tts], T.fsend[:, 64 * tts[0]:64 * tts[-1] + 64], banks[k][:, 0:64 * len(tts)]
        e = V(w, cp, o, i) if q == "V" else act(w, o, i, F.Copy)
        use("G", [e])
        n = len(eng) // len(tts)
        g.remote_dma_fused([RemoteDMATransfer(dst_ids=[dst_id(order[t])], dma_engine_mask=bits(eng[n * i:n * i + n]), remote_sem=T.sem["far%d" % k],
                                              srcs=[T.fsend[:, 64 * t:64 * t + 64]], dsts=[T.fland[:, 64 * rank:64 * rank + 64]])
                            for i, t in enumerate(tts)], local_sem=T.sem.fsent)

    for step in PLAN:
        if step == "lists":
            e_sel.append(lists(1))
        elif len(step) == 2:
            send(*step)
        else:
            gather(*step)
            for u in range(4 * (N - 1)):
                if u not in summed and sum(max(0, min(j1, 128 * u + 128) - max(j0, 128 * u)) for j0, j1, e in gathered) == 128:
                    sensors(u)
    e_w1 = chain([e_ac, e_idf, e_sel[0]], [lambda: pe.matmul(p[6][0:1, 0:16], ac, T.identf[0:16, 0:16], start=True, stop=True)])
    early = 1
    for k in range(early):
        collect(k)
    for u in range(4 * (N - 1), 4 * N):
        sensors(u)
    e_w2 = V([e_w1, e_wc], tt, T.w2[0:1, :], p[6][0:1, 0:16], T.wc[0:1, :], A.add)
    e_w = run("Y", [e_w2], lambda: g.sync.dma_start(T.w[:, :], T.w2[0:1, :]), inc=16)

    for k in range(early, len(GROUPS) - 1):
        collect(k)
    e_fin = run("P", [], lambda: last[0])
    use("V", [e_fin])
    vec.wait_ge(T.sem["far%d" % (len(GROUPS) - 1)], len(eng))
    e_y = V([], tt, T.ysb[:, :], p[5][:, 0:64], T.fland[:, 64 * mate:64 * mate + 64], A.add)
    e_st = event()
    for h in range(2):
        run("YS"[h], [e_y], lambda: (g.sync, sca)[h].dma_start(T.y[:, 256 * h:256 * h + 256], T.ysb[64 * h:64 * h + 64, :]), ev=e_st, inc=16)
    use("Y", [e_w, e_st])
    g.wait_ge(T.sem.ssent, len(eng))
    g.wait_ge(T.sem.csent, len(eng))
    g.wait_ge(T.sem.fsent, len(GROUPS) * len(eng))
    for e in events:
        if not e["used"]:
            g.wait_ge(e["sem"], e["total"])
